import numpy as np
import ml_dtypes


def mxq(x, axis, fmt="e4m3"):
    dtype, down = {"e4m3": (ml_dtypes.float8_e4m3fn, 7), "e5m2": (ml_dtypes.float8_e5m2, 14)}[fmt]
    v = np.moveaxis(np.asarray(x, np.float32).astype(ml_dtypes.bfloat16).astype(np.float64), axis, -1)
    blocks = v.reshape(v.shape[:-1] + (-1, 32))
    amax = np.abs(blocks).max(-1, keepdims=True)
    byte = np.maximum(np.where(amax > 0, np.frexp(amax)[1] - 1 + 127, 0) - down, 1)
    scale = np.exp2(byte - 127.0)
    codes = (blocks / scale).astype(np.float32).astype(dtype).astype(np.float64)
    return np.moveaxis((codes * scale).reshape(v.shape), -1, axis)


WIDE = False


def mx_kscale(k):
    if not WIDE:
        return np.ones(k)
    levels = np.array([24, -24, 12, -12, 0])
    if k % 512:
        return np.exp2(np.random.permutation(np.resize(levels, k // 32))).repeat(32)
    a = np.empty((k // 512, 16))
    for p in range(k // 512):
        a[p, :8] = np.random.permutation(np.resize(levels, 8))
        for g in range(8):
            far = levels[np.abs(levels - a[p, g]) >= 10]
            a[p, g + 8] = far[np.random.randint(len(far))]
    return np.exp2(a.ravel()).repeat(32)


def f64(x):
    return np.asarray(x).astype(np.float64)


def striped(idx):
    return np.tile(idx.reshape(-1, 16).T, (8, 1)).astype(np.uint16)


def unstriped(offs):
    return offs[:16].T.reshape(-1).astype(np.int64)


E2M1 = np.array([0.0, 0.5, 1.0, 1.5, 2.0, 3.0, 4.0, 6.0, -0.0, -0.5, -1.0, -1.5, -2.0, -3.0, -4.0, -6.0])


def pack_weight(w, fmt):
    k, n = w.shape
    w = f64(np.asarray(w, np.float32).astype(ml_dtypes.bfloat16)).reshape(k // 32, 32, n)
    amax = np.abs(w).max(1)
    if fmt == "e4m3":
        byte = np.frexp(amax)[1] - 1 + 127 - 7
    else:
        mant, ex = np.frexp(amax / 6.0)
        byte = np.where(mant > 0.5, ex, ex - 1) + 127
    byte = np.clip(np.where(amax > 0, byte, 1), 1, 254)
    scaled = (w * np.exp2(127.0 - byte)[:, None, :]).reshape(k, n).astype(np.float32)
    by_word = np.ascontiguousarray(scaled.reshape(k // 512, 128, 4, n).transpose(0, 1, 3, 2))
    if fmt == "e4m3":
        words = by_word.astype(ml_dtypes.float8_e4m3fn).view(np.uint8)
    else:
        c = by_word.astype(ml_dtypes.float4_e2m1fn).view(np.uint8) & 0xF
        words = (c[..., 0::2] | (c[..., 1::2] << 4)).reshape(k // 512, 128, 2 * n)
    return np.ascontiguousarray(words), np.ascontiguousarray(byte.astype(np.uint8).reshape(k // 512, 16, n))


def unpack_weight(words, scales, fmt):
    g, _, n = scales.shape
    words = np.ascontiguousarray(words).reshape(g, 128, n, -1)
    if fmt == "e4m3":
        vals = words.view(ml_dtypes.float8_e4m3fn).astype(np.float64)
    else:
        nib = np.empty((g, 128, n, 4), np.uint8)
        nib[..., 0::2] = words & 0xF
        nib[..., 1::2] = words >> 4
        vals = E2M1[nib]
    vals = vals * np.repeat(np.exp2(scales.astype(np.float64) - 127.0), 8, axis=1)[..., None]
    return vals.transpose(0, 1, 3, 2).reshape(g * 512, n)


K, L, R, N, T, J = 512, 512, 512, 256, 4096, 1024


def setup_inputs():
    n = np.random.standard_normal
    s = mx_kscale(K)[:, None]
    s2 = mx_kscale(L)[:, None]
    u = mx_kscale(R)[:, None]
    p_tab = pack_weight(n((K, T)) * s, "e4m3")
    p_tab2 = pack_weight(n((L, T)) * s2, "e4m3")
    p_wer = pack_weight(n((K, R)) / np.sqrt(K) / s * u.T, "e2m1")
    p_wei = pack_weight(n((K, R)) / np.sqrt(K) / s * u.T, "e2m1")
    p_wrr = pack_weight(n((L, R)) / np.sqrt(L) / s2, "e2m1")
    p_wri = pack_weight(n((L, R)) / np.sqrt(L) / s2, "e2m1")
    return {
        "tab_words": p_tab[0],
        "tab_scales": p_tab[1],
        "tab2_words": p_tab2[0],
        "tab2_scales": p_tab2[1],
        "wer_words": p_wer[0],
        "wer_scales": p_wer[1],
        "wei_words": p_wei[0],
        "wei_scales": p_wei[1],
        "wrr_words": p_wrr[0],
        "wrr_scales": p_wrr[1],
        "wri_words": p_wri[0],
        "wri_scales": p_wri[1],
        "nr": (n((R, N)) / np.sqrt(R) / u).astype(np.float32),
        "ni": (n((R, N)) / np.sqrt(R) / u).astype(np.float32),
        "offs": striped(np.random.permutation(T)[:J]),
        "offs2": striped(np.random.permutation(T)[:J]),
    }


def reference(tab_words, tab_scales, tab2_words, tab2_scales, wer_words, wer_scales, wei_words, wei_scales, wrr_words, wrr_scales, wri_words, wri_scales, nr, ni, offs, offs2):
    idx = unstriped(offs)
    idx2 = unstriped(offs2)
    tab_ = unpack_weight(tab_words, tab_scales, "e4m3")[:, idx]
    tab2_ = unpack_weight(tab2_words, tab2_scales, "e4m3")[:, idx2]
    wer_ = unpack_weight(wer_words, wer_scales, "e2m1")
    aer = wer_.T @ tab_
    wei_ = unpack_weight(wei_words, wei_scales, "e2m1")
    aei = wei_.T @ tab_
    wrr_ = unpack_weight(wrr_words, wrr_scales, "e2m1")
    arr = wrr_.T @ tab2_
    wri_ = unpack_weight(wri_words, wri_scales, "e2m1")
    ari = wri_.T @ tab2_
    hr = aer * arr - aei * ari
    hi = aer * ari + aei * arr
    hr_ = mxq(hr, 0, "e4m3")
    hi_ = mxq(hi, 0, "e4m3")
    nr_ = mxq(f64(nr), 0, "e4m3")
    ni_ = mxq(f64(ni), 0, "e4m3")
    y = nr_.T @ hr_ + ni_.T @ hi_
    return y

@@ -1,0 +1,201 @@
+from contextlib import ExitStack
+
+import concourse.mybir as mybir
+from concourse.masks import make_identity
+
+K, L, R, N, T, J = 512, 512, 512, 256, 4096, 1024
+FLOPS = 2 * 4 * K * R * J + 2 * 2 * R * N * J
+
+F32 = mybir.dt.float32
+BF16 = mybir.dt.bfloat16
+I32 = mybir.dt.int32
+U32 = mybir.dt.uint32
+U16 = mybir.dt.uint16
+U8 = mybir.dt.uint8
+FP8X4 = mybir.dt.float8_e4m3fn_x4
+FP4X4 = mybir.dt.float4_e2m1fn_x4
+MULT = mybir.AluOpType.mult
+ADD = mybir.AluOpType.add
+
+P = 128
+PACK = 4
+HALF = J // 2
+TILES = J // P
+AHEAD = 3
+GROUPS = ((0, 1), (2, 3), (4, 5), (6,), (7,))
+GROUP_OF = {jt: g for g, tiles in enumerate(GROUPS) for jt in tiles}
+
+
+def tile_list_ckg_none_kernel(tc, tab_words, tab_scales, tab2_words, tab2_scales, wer_words, wer_scales, wei_words,
+        wei_scales, wrr_words, wrr_scales, wri_words, wri_scales, nr, ni, offs, offs2, out):
+    nc = tc.nc
+    with ExitStack() as ctx:
+        keep = ctx.enter_context(tc.tile_pool(name="keep", bufs=1))
+        big = ctx.enter_context(tc.tile_pool(name="big", bufs=1))
+        ring = ctx.enter_context(tc.tile_pool(name="ring", bufs=2))
+        psum = ctx.enter_context(tc.psum_pool(name="psum", bufs=1))
+
+        lists = [keep.tile([P, J // 16], U16, name=f"list{i}") for i in range(2)]
+        words = [big.tile([P, T], I32, name=f"words{i}", align_bytes=64, offset=4 * T * i) for i in range(2)]
+        planes = [big.tile([P, T], U8, name=f"plane{i}", align_bytes=64, offset=8 * T + T * i) for i in range(2)]
+        w_words = [keep.tile([P, 2 * R], U8, name=f"w_words{i}", align_bytes=64) for i in range(2)]
+        w_plane = keep.tile([P, 4 * R], U8, name="w_plane", align_bytes=64)
+        t_plane = keep.tile([P, 2 * J], U8, name="t_plane", align_bytes=64)
+        ident = keep.tile([P, P], F32, name="ident")
+
+        nc.vector.memset(planes[0][:].bitcast(I32), 0)
+        nc.vector.memset(planes[1][:].bitcast(I32), 0)
+        nc.vector.memset(t_plane[:].bitcast(I32), 0)
+        nc.gpsimd.memset(w_plane[:].bitcast(I32), 0)
+
+        def load_w(queue, i, src):
+            queue.dma_start(out=w_words[i][:].bitcast(I32), in_=src[0].bitcast(I32))
+
+        nc.sync.dma_start(lists[0][:], offs)
+        nc.sync.dma_start(lists[1][:], offs2)
+        nc.sync.dma_start(out=words[0][:], in_=tab_words[0].rearrange("p t i -> p (t i)").bitcast(I32))
+        load_w(nc.sync, 0, wer_words)
+        load_w(nc.sync, 1, wei_words)
+        nc.sync.dma_start(out=words[1][:], in_=tab2_words[0].rearrange("p t i -> p (t i)").bitcast(I32))
+        for i, src in enumerate((tab_scales, tab2_scales)):
+            nc.scalar.dma_start(out=planes[i][0:P:8, :].bitcast(I32), in_=src[0].bitcast(I32))
+
+        for i, src in enumerate((wer_scales, wei_scales, wrr_scales, wri_scales)):
+            nc.gpsimd.dma_start(out=w_plane[0:P:8, i * R : (i + 1) * R].bitcast(I32), in_=src[0].bitcast(I32))
+        for r in range(1, 4):
+            nc.gpsimd.dma_start(out=w_plane[r:P:32, :].bitcast(I32), in_=w_plane[8 * r : P : 32, :].bitcast(I32))
+        make_identity(nc, ident[:])
+
+        g_words = {}
+        g_plane = keep.tile([P, 2 * J], U8, name="g_plane", align_bytes=64)
+
+        def gather_words(i, h):
+            cols = HALF // 16
+            g_words[i, h] = big.tile([P, HALF], U32, name=f"g_words{i}{h}", align_bytes=64,
+                                     offset=8 * T + T * (1 - i) + 4 * HALF * h)
+            nc.vector.tensor_copy(g_words[i, h][:], words[i][:].bitcast(U32).indirect(lists[i][:, h * cols : (h + 1) * cols]))
+
+        for i in range(2):
+            nc.vector.tensor_copy(g_plane[:, i * J : (i + 1) * J], planes[i][:].indirect(lists[i][:]))
+        for r in range(4):
+            nc.scalar.dma_start(out=t_plane[r:P:32, :].bitcast(I32), in_=g_plane[8 * r : P : 32, :].bitcast(I32))
+        gather_words(0, 0)
+        gather_words(0, 1)
+        for i, src in enumerate((wrr_words, wri_words)):
+            w_words.append(big.tile([P, 2 * R], U8, name=f"w_late{i}", align_bytes=64, offset=2 * R * i))
+            load_w(nc.sync, 2 + i, src)
+        n_raw = [big.tile([P, PACK, N], F32, name=f"n_raw{i}", align_bytes=64, offset=4 * R + 16 * N * i) for i in range(2)]
+        for i, src in enumerate((nr, ni)):
+            nc.sync.dma_start(out=n_raw[i][:], in_=src.rearrange("(p t) n -> p t n", t=PACK))
+        gather_words(1, 0)
+        gather_words(1, 1)
+
+        n_bf = keep.tile([P, 2, N, PACK], BF16, name="n_bf", align_bytes=64)
+        n_codes = keep.tile([P, 2 * N], U32, name="n_codes", align_bytes=64)
+        n_plane = keep.tile([P, 2 * N], U8, name="n_plane", align_bytes=64)
+
+        def project(tab, w, jt, bank):
+            h, c = divmod(jt * P, HALF)
+            nc.tensor.matmul_mx(out=bank[:], lhsT=g_words[tab, h][:, c : c + P].bitcast(FP8X4),
+                                lhsT_scale=t_plane[:, tab * J + jt * P : tab * J + (jt + 1) * P],
+                                rhs=w_words[w][:].bitcast(FP4X4), rhs_scale=w_plane[:, w * R : (w + 1) * R],
+                                start=True, stop=True)
+
+        def by_slot(bank):
+            return bank[:].rearrange("j (p t) -> j t p", t=PACK)
+
+        ent = {}
+        rel = {}
+        prods = {}
+        h_bf = {}
+        h_q = {}
+
+        def entity(jt):
+            ent[jt] = ring.tile([P, 2, PACK, P], F32, name="ent", bufs=AHEAD + 1)
+            for c in range(2):
+                bank = psum.tile([P, R], F32, name="e_bank", bufs=2)
+                project(0, c, jt, bank)
+                nc.scalar.copy(ent[jt][:, c], by_slot(bank))
+
+        def relation(jt):
+            rel[jt] = []
+            for c in range(2):
+                bank = psum.tile([P, R], F32, name="r_bank", bufs=3)
+                project(1, 2 + c, jt, bank)
+                rel[jt].append(bank)
+
+        def products(jt):
+            pa = ring.tile([P, 2, PACK, P], F32, name="pa", bufs=3)
+            pb = ring.tile([P, PACK, P], F32, name="pb", bufs=3)
+            pc = ring.tile([P, PACK, P], F32, name="pc", bufs=3)
+            arr, ari = by_slot(rel[jt][0]), by_slot(rel[jt][1])
+            nc.vector.tensor_tensor(pa[:], arr.unsqueeze(1).to_broadcast([P, 2, PACK, P]), ent[jt][:], MULT)
+            nc.vector.scalar_tensor_tensor(pb[:], ari, -1.0, ent[jt][:, 1], MULT, MULT)
+            nc.vector.tensor_tensor(pc[:], ari, ent[jt][:, 0], MULT)
+            prods[jt] = ((pa[:, 0], pb[:]), (pa[:, 1], pc[:]))
+
+        def turn(jt):
+            g = GROUP_OF[jt]
+            jj = jt - GROUPS[g][0]
+            if jj == 0:
+                h_bf[g] = ring.tile([P, 2, len(GROUPS[g]) * P, PACK], BF16, name="h_bf", align_bytes=64)
+            for c in range(2):
+                bank = psum.tile([P, PACK, P], F32, name="h_bank", bufs=2)
+                for s in range(2):
+                    for t in range(PACK):
+                        nc.tensor.matmul(bank[:, t, :], prods[jt][c][s][:, t, :], ident[:], is_transpose=True,
+                                         start=(s == 0 and t == 0), stop=(s == 1 and t == PACK - 1))
+                nc.scalar.copy(h_bf[g][:, c, jj * P : (jj + 1) * P, :], bank[:].rearrange("p t j -> p j t"))
+
+        def quantise(g):
+            W = len(GROUPS[g]) * P
+            codes = ring.tile([P, 2, W], U32, name="h_codes", align_bytes=64)
+            plane = ring.tile([P, 2, W], U8, name="h_plane", align_bytes=64)
+            if g == len(GROUPS) - 1:
+                for c in range(2):
+                    nc.vector.quantize_mx(out=codes[:, c, :].bitcast(FP8X4), scales=plane[:, c, :],
+                                          in_=h_bf[g][:, c].rearrange("p j t -> p (j t)"))
+            else:
+                nc.vector.quantize_mx(out=codes[:].rearrange("p c j -> p (c j)").bitcast(FP8X4),
+                                      scales=plane[:].rearrange("p c j -> p (c j)"),
+                                      in_=h_bf[g][:].rearrange("p c j t -> p (c j t)"))
+            h_q[g] = (codes, plane)
+
+        def score(g):
+            codes, plane = h_q[g]
+            W = len(GROUPS[g]) * P
+            j0 = GROUPS[g][0] * P
+            bank = psum.tile([P, 2, W], F32, name="y_bank", bufs=1)
+            for c in range(2):
+                for nt in range(2):
+                    cols = slice(c * N + nt * P, c * N + (nt + 1) * P)
+                    nc.tensor.matmul_mx(out=bank[:, nt, :], lhsT=n_codes[:, cols].bitcast(FP8X4), lhsT_scale=n_plane[:, cols],
+                                        rhs=codes[:, c, :].bitcast(FP8X4), rhs_scale=plane[:, c, :],
+                                        start=(c == 0 and nt == 0), stop=(c == 1 and nt == 1))
+            y = ring.tile([P, 2, W], F32, name="y")
+            nc.scalar.copy(y[:], bank[:])
+            nc.sync.dma_start(out=out.rearrange("(nt p) j -> p nt j", p=P)[:, :, j0 : j0 + W], in_=y[:])
+
+        for jt in range(AHEAD):
+            entity(jt)
+        relation(0)
+        for i in range(2):
+            nc.gpsimd.tensor_scalar(n_bf[:, i], n_raw[i][:].rearrange("p t n -> p n t"), 1.0, 0.0, MULT, ADD)
+        for jt in range(TILES + 2):
+            if jt < TILES:
+                products(jt)
+            if jt == 2:
+                nc.vector.quantize_mx(out=n_codes[:].bitcast(FP8X4), scales=n_plane[:],
+                                      in_=n_bf[:].rearrange("p c n t -> p (c n t)"))
+            if 1 <= jt <= TILES:
+                turn(jt - 1)
+            if jt + 1 < TILES:
+                relation(jt + 1)
+            if jt + AHEAD < TILES:
+                entity(jt + AHEAD)
+            for g in range(len(GROUPS)):
+                if GROUPS[g][-1] + 2 == jt:
+                    score(g)
+            for g in range(len(GROUPS)):
+                if GROUPS[g][-1] + 1 == jt:
+                    quantise(g)

@@ -1,7 +1,6 @@
 from contextlib import ExitStack
 
 import concourse.mybir as mybir
-from concourse.masks import make_identity
 
 K, L, R, N, T, J = 512, 512, 512, 256, 4096, 1024
 FLOPS = 2 * 4 * K * R * J + 2 * 2 * R * N * J
@@ -21,7 +20,7 @@ P = 128
 PACK = 4
 HALF = J // 2
 TILES = J // P
-AHEAD = 3
+AHEAD = 2
 GROUPS = ((0, 1), (2, 3), (4, 5), (6,), (7,))
 GROUP_OF = {jt: g for g, tiles in enumerate(GROUPS) for jt in tiles}
 
@@ -38,33 +37,25 @@ def tile_list_ckg_none_kernel(tc, tab_words, tab_scales, tab2_words, tab2_scales
         lists = [keep.tile([P, J // 16], U16, name=f"list{i}") for i in range(2)]
         words = [big.tile([P, T], I32, name=f"words{i}", align_bytes=64, offset=4 * T * i) for i in range(2)]
         planes = [big.tile([P, T], U8, name=f"plane{i}", align_bytes=64, offset=8 * T + T * i) for i in range(2)]
-        w_words = [keep.tile([P, 2 * R], U8, name=f"w_words{i}", align_bytes=64) for i in range(2)]
-        w_plane = keep.tile([P, 4 * R], U8, name="w_plane", align_bytes=64)
-        t_plane = keep.tile([P, 2 * J], U8, name="t_plane", align_bytes=64)
-        ident = keep.tile([P, P], F32, name="ident")
+        w_raw = keep.tile([P, 4, R // 2], I32, name="w_raw", align_bytes=64)
+        w_words = keep.tile([P, 4, PACK, P // 2], I32, name="w_words", align_bytes=64)
+        s_raw = keep.tile([P, 4, R // 4], I32, name="s_raw", align_bytes=64)
+        plane_all = keep.tile([P, 4 * R + 2 * J], U8, name="plane_all", align_bytes=64)
 
+        nc.gpsimd.memset(s_raw[:], 0)
         nc.vector.memset(planes[0][:].bitcast(I32), 0)
         nc.vector.memset(planes[1][:].bitcast(I32), 0)
-        nc.vector.memset(t_plane[:].bitcast(I32), 0)
-        nc.gpsimd.memset(w_plane[:].bitcast(I32), 0)
-
-        def load_w(queue, i, src):
-            queue.dma_start(out=w_words[i][:].bitcast(I32), in_=src[0].bitcast(I32))
 
         nc.sync.dma_start(lists[0][:], offs)
         nc.sync.dma_start(lists[1][:], offs2)
         nc.sync.dma_start(out=words[0][:], in_=tab_words[0].rearrange("p t i -> p (t i)").bitcast(I32))
-        load_w(nc.sync, 0, wer_words)
-        load_w(nc.sync, 1, wei_words)
+        for i, src in enumerate((wer_words, wei_words, wrr_words, wri_words)):
+            nc.sync.dma_start(out=w_raw[:, i, :], in_=src[0].bitcast(I32))
         nc.sync.dma_start(out=words[1][:], in_=tab2_words[0].rearrange("p t i -> p (t i)").bitcast(I32))
         for i, src in enumerate((tab_scales, tab2_scales)):
             nc.scalar.dma_start(out=planes[i][0:P:8, :].bitcast(I32), in_=src[0].bitcast(I32))
-
         for i, src in enumerate((wer_scales, wei_scales, wrr_scales, wri_scales)):
-            nc.gpsimd.dma_start(out=w_plane[0:P:8, i * R : (i + 1) * R].bitcast(I32), in_=src[0].bitcast(I32))
-        for r in range(1, 4):
-            nc.gpsimd.dma_start(out=w_plane[r:P:32, :].bitcast(I32), in_=w_plane[8 * r : P : 32, :].bitcast(I32))
-        make_identity(nc, ident[:])
+            nc.gpsimd.dma_start(out=s_raw[0:P:8, i, :], in_=src[0].bitcast(I32))
 
         g_words = {}
         g_plane = keep.tile([P, 2 * J], U8, name="g_plane", align_bytes=64)
@@ -77,16 +68,19 @@ def tile_list_ckg_none_kernel(tc, tab_words, tab_scales, tab2_words, tab2_scales
 
         for i in range(2):
             nc.vector.tensor_copy(g_plane[:, i * J : (i + 1) * J], planes[i][:].indirect(lists[i][:]))
-        for r in range(4):
-            nc.scalar.dma_start(out=t_plane[r:P:32, :].bitcast(I32), in_=g_plane[8 * r : P : 32, :].bitcast(I32))
+        nc.vector.tensor_copy(plane_all[:, 0 : 4 * R].bitcast(I32).rearrange("p (w t m) -> p w t m", w=4, t=PACK),
+                              s_raw[:].rearrange("p w (m t) -> p w t m", t=PACK))
+        nc.vector.tensor_copy(plane_all[:, 4 * R :].bitcast(I32), g_plane[:].bitcast(I32))
+        for r in range(1, 4):
+            nc.scalar.dma_start(out=plane_all[r:P:32, :].bitcast(I32), in_=plane_all[8 * r : P : 32, :].bitcast(I32))
+        nc.vector.tensor_copy(w_words[:].rearrange("p w t (m k) -> p w t m k", k=2),
+                              w_raw[:].rearrange("p w (m t k) -> p w t m k", t=PACK, k=2))
         gather_words(0, 0)
         gather_words(0, 1)
-        for i, src in enumerate((wrr_words, wri_words)):
-            w_words.append(big.tile([P, 2 * R], U8, name=f"w_late{i}", align_bytes=64, offset=2 * R * i))
-            load_w(nc.sync, 2 + i, src)
-        n_raw = [big.tile([P, PACK, N], F32, name=f"n_raw{i}", align_bytes=64, offset=4 * R + 16 * N * i) for i in range(2)]
-        for i, src in enumerate((nr, ni)):
-            nc.sync.dma_start(out=n_raw[i][:], in_=src.rearrange("(p t) n -> p t n", t=PACK))
+        n_raw = [big.tile([P, PACK, N], F32, name=f"n_raw{i}", align_bytes=64, offset=16 * N * i) for i in range(2)]
+        for c, src in enumerate((nr, ni)):
+            for i in range(4):
+                nc.sync.dma_start(out=n_raw[c][i:P:4], in_=src.rearrange("(m t i) n -> i m t n", t=PACK, i=4)[i])
         gather_words(1, 0)
         gather_words(1, 1)
 
@@ -96,13 +90,15 @@ def tile_list_ckg_none_kernel(tc, tab_words, tab_scales, tab2_words, tab2_scales
 
         def project(tab, w, jt, bank):
             h, c = divmod(jt * P, HALF)
-            nc.tensor.matmul_mx(out=bank[:], lhsT=g_words[tab, h][:, c : c + P].bitcast(FP8X4),
-                                lhsT_scale=t_plane[:, tab * J + jt * P : tab * J + (jt + 1) * P],
-                                rhs=w_words[w][:].bitcast(FP4X4), rhs_scale=w_plane[:, w * R : (w + 1) * R],
-                                start=True, stop=True)
+            s0 = 4 * R + tab * J + jt * P
+            for t in range(PACK):
+                nc.tensor.matmul_mx(out=bank[:, t, :], lhsT=w_words[:, w, t, :].bitcast(U8).bitcast(FP4X4),
+                                    lhsT_scale=plane_all[:, w * R + t * P : w * R + (t + 1) * P],
+                                    rhs=g_words[tab, h][:, c : c + P].bitcast(FP8X4), rhs_scale=plane_all[:, s0 : s0 + P],
+                                    start=True, stop=True)
 
-        def by_slot(bank):
-            return bank[:].rearrange("j (p t) -> j t p", t=PACK)
+        def woven(bank):
+            return bank[:].rearrange("p t j -> p j t")
 
         ent = {}
         rel = {}
@@ -111,91 +107,79 @@ def tile_list_ckg_none_kernel(tc, tab_words, tab_scales, tab2_words, tab2_scales
         h_q = {}
 
         def entity(jt):
-            ent[jt] = ring.tile([P, 2, PACK, P], F32, name="ent", bufs=AHEAD + 1)
+            ent[jt] = ring.tile([P, 2, P, PACK], F32, name="ent", bufs=AHEAD + 1)
             for c in range(2):
-                bank = psum.tile([P, R], F32, name="e_bank", bufs=2)
+                bank = psum.tile([P, PACK, P], F32, name="e_bank", bufs=2)
                 project(0, c, jt, bank)
-                nc.scalar.copy(ent[jt][:, c], by_slot(bank))
+                nc.scalar.copy(ent[jt][:, c], woven(bank))
 
         def relation(jt):
             rel[jt] = []
             for c in range(2):
-                bank = psum.tile([P, R], F32, name="r_bank", bufs=3)
+                bank = psum.tile([P, PACK, P], F32, name="r_bank", bufs=4)
                 project(1, 2 + c, jt, bank)
                 rel[jt].append(bank)
 
         def products(jt):
-            pa = ring.tile([P, 2, PACK, P], F32, name="pa", bufs=3)
-            pb = ring.tile([P, PACK, P], F32, name="pb", bufs=3)
-            pc = ring.tile([P, PACK, P], F32, name="pc", bufs=3)
-            arr, ari = by_slot(rel[jt][0]), by_slot(rel[jt][1])
-            nc.vector.tensor_tensor(pa[:], arr.unsqueeze(1).to_broadcast([P, 2, PACK, P]), ent[jt][:], MULT)
-            nc.vector.scalar_tensor_tensor(pb[:], ari, -1.0, ent[jt][:, 1], MULT, MULT)
-            nc.vector.tensor_tensor(pc[:], ari, ent[jt][:, 0], MULT)
-            prods[jt] = ((pa[:, 0], pb[:]), (pa[:, 1], pc[:]))
+            pa = ring.tile([P, 2, P, PACK], F32, name="pa", bufs=3)
+            pb = ring.tile([P, 2, P, PACK], F32, name="pb", bufs=3)
+            arr, ari = woven(rel[jt][0]), woven(rel[jt][1])
+            nc.vector.tensor_tensor(pa[:], arr.unsqueeze(1).to_broadcast([P, 2, P, PACK]), ent[jt][:], MULT)
+            nc.vector.scalar_tensor_tensor(pb[:, 0], ari, -1.0, ent[jt][:, 1], MULT, MULT)
+            nc.vector.tensor_tensor(pb[:, 1], ari, ent[jt][:, 0], MULT)
+            prods[jt] = (pa, pb)
 
         def turn(jt):
             g = GROUP_OF[jt]
             jj = jt - GROUPS[g][0]
             if jj == 0:
-                h_bf[g] = ring.tile([P, 2, len(GROUPS[g]) * P, PACK], BF16, name="h_bf", align_bytes=64)
-            for c in range(2):
-                bank = psum.tile([P, PACK, P], F32, name="h_bank", bufs=2)
-                for s in range(2):
-                    for t in range(PACK):
-                        nc.tensor.matmul(bank[:, t, :], prods[jt][c][s][:, t, :], ident[:], is_transpose=True,
-                                         start=(s == 0 and t == 0), stop=(s == 1 and t == PACK - 1))
-                nc.scalar.copy(h_bf[g][:, c, jj * P : (jj + 1) * P, :], bank[:].rearrange("p t j -> p j t"))
+                h_bf[g] = ring.tile([P, 2, len(GROUPS[g]) * P, PACK], BF16, name="h_bf", align_bytes=64, bufs=3)
+            engine = nc.vector if jt == TILES - 1 else nc.gpsimd
+            engine.tensor_tensor(h_bf[g][:, :, jj * P : (jj + 1) * P, :], prods[jt][0][:], prods[jt][1][:], ADD)
 
         def quantise(g):
             W = len(GROUPS[g]) * P
             codes = ring.tile([P, 2, W], U32, name="h_codes", align_bytes=64)
             plane = ring.tile([P, 2, W], U8, name="h_plane", align_bytes=64)
-            if g == len(GROUPS) - 1:
-                for c in range(2):
-                    nc.vector.quantize_mx(out=codes[:, c, :].bitcast(FP8X4), scales=plane[:, c, :],
-                                          in_=h_bf[g][:, c].rearrange("p j t -> p (j t)"))
-            else:
-                nc.vector.quantize_mx(out=codes[:].rearrange("p c j -> p (c j)").bitcast(FP8X4),
-                                      scales=plane[:].rearrange("p c j -> p (c j)"),
-                                      in_=h_bf[g][:].rearrange("p c j t -> p (c j t)"))
+            nc.vector.quantize_mx(out=codes[:].rearrange("p c j -> p (c j)").bitcast(FP8X4),
+                                  scales=plane[:].rearrange("p c j -> p (c j)"),
+                                  in_=h_bf[g][:].rearrange("p c j t -> p (c j t)"))
             h_q[g] = (codes, plane)
 
         def score(g):
             codes, plane = h_q[g]
             W = len(GROUPS[g]) * P
             j0 = GROUPS[g][0] * P
-            bank = psum.tile([P, 2, W], F32, name="y_bank", bufs=1)
+            bank = psum.tile([P, 2, W], F32, name="y_bank", bufs=2)
             for c in range(2):
                 for nt in range(2):
                     cols = slice(c * N + nt * P, c * N + (nt + 1) * P)
                     nc.tensor.matmul_mx(out=bank[:, nt, :], lhsT=n_codes[:, cols].bitcast(FP8X4), lhsT_scale=n_plane[:, cols],
                                         rhs=codes[:, c, :].bitcast(FP8X4), rhs_scale=plane[:, c, :],
                                         start=(c == 0 and nt == 0), stop=(c == 1 and nt == 1))
-            y = ring.tile([P, 2, W], F32, name="y")
+            y = ring.tile([P, 2, W], F32, name="y", bufs=len(GROUPS))
             nc.scalar.copy(y[:], bank[:])
             nc.sync.dma_start(out=out.rearrange("(nt p) j -> p nt j", p=P)[:, :, j0 : j0 + W], in_=y[:])
 
         for jt in range(AHEAD):
             entity(jt)
         relation(0)
-        for i in range(2):
-            nc.gpsimd.tensor_scalar(n_bf[:, i], n_raw[i][:].rearrange("p t n -> p n t"), 1.0, 0.0, MULT, ADD)
         for jt in range(TILES + 2):
             if jt < TILES:
                 products(jt)
-            if jt == 2:
-                nc.vector.quantize_mx(out=n_codes[:].bitcast(FP8X4), scales=n_plane[:],
-                                      in_=n_bf[:].rearrange("p c n t -> p (c n t)"))
-            if 1 <= jt <= TILES:
-                turn(jt - 1)
             if jt + 1 < TILES:
                 relation(jt + 1)
             if jt + AHEAD < TILES:
                 entity(jt + AHEAD)
+            if jt == 1:
+                for c in range(2):
+                    nc.scalar.copy(n_bf[:, c], n_raw[c][:].rearrange("p t n -> p n t"))
+            if jt == 3:
+                nc.vector.quantize_mx(out=n_codes[:].bitcast(FP8X4), scales=n_plane[:],
+                                      in_=n_bf[:].rearrange("p c n t -> p (c n t)"))
+            if jt < TILES:
+                turn(jt)
             for g in range(len(GROUPS)):
-                if GROUPS[g][-1] + 2 == jt:
-                    score(g)
-            for g in range(len(GROUPS)):
-                if GROUPS[g][-1] + 1 == jt:
+                if min(GROUPS[g][-1] + 2, TILES) == jt:
                     quantise(g)
+                    score(g)

@@ -21,6 +21,7 @@ PACK = 4
 HALF = J // 2
 TILES = J // P
 AHEAD = 2
+G_AT = ((10 * T + 2 * R, 11 * T), (8 * T, 9 * T))
 GROUPS = ((0, 1), (2, 3), (4, 5), (6,), (7,))
 GROUP_OF = {jt: g for g, tiles in enumerate(GROUPS) for jt in tiles}
 
@@ -37,33 +38,35 @@ def tile_list_ckg_none_kernel(tc, tab_words, tab_scales, tab2_words, tab2_scales
         lists = [keep.tile([P, J // 16], U16, name=f"list{i}") for i in range(2)]
         words = [big.tile([P, T], I32, name=f"words{i}", align_bytes=64, offset=4 * T * i) for i in range(2)]
         planes = [big.tile([P, T], U8, name=f"plane{i}", align_bytes=64, offset=8 * T + T * i) for i in range(2)]
-        w_raw = keep.tile([P, 4, R // 2], I32, name="w_raw", align_bytes=64)
+        w_raw = big.tile([P, 4, R // 2], I32, name="w_raw", align_bytes=64, offset=11 * T)
         w_words = keep.tile([P, 4, PACK, P // 2], I32, name="w_words", align_bytes=64)
-        s_raw = keep.tile([P, 4, R // 4], I32, name="s_raw", align_bytes=64)
+        s_raw = big.tile([P, 4, R // 4], I32, name="s_raw", align_bytes=64, offset=10 * T)
         plane_all = keep.tile([P, 4 * R + 2 * J], U8, name="plane_all", align_bytes=64)
 
-        nc.gpsimd.memset(s_raw[:], 0)
         nc.vector.memset(planes[0][:].bitcast(I32), 0)
-        nc.vector.memset(planes[1][:].bitcast(I32), 0)
+        nc.gpsimd.memset(planes[1][:].bitcast(I32), 0)
+        nc.vector.memset(s_raw[:], 0)
 
+        w_src = (wer_words, wei_words, wrr_words, wri_words)
         nc.sync.dma_start(lists[0][:], offs)
         nc.sync.dma_start(lists[1][:], offs2)
-        nc.sync.dma_start(out=words[0][:], in_=tab_words[0].rearrange("p t i -> p (t i)").bitcast(I32))
-        for i, src in enumerate((wer_words, wei_words, wrr_words, wri_words)):
-            nc.sync.dma_start(out=w_raw[:, i, :], in_=src[0].bitcast(I32))
-        nc.sync.dma_start(out=words[1][:], in_=tab2_words[0].rearrange("p t i -> p (t i)").bitcast(I32))
+        for i in range(3):
+            nc.sync.dma_start(out=w_raw[:, i, :], in_=w_src[i][0].bitcast(I32))
         for i, src in enumerate((tab_scales, tab2_scales)):
-            nc.scalar.dma_start(out=planes[i][0:P:8, :].bitcast(I32), in_=src[0].bitcast(I32))
+            nc.sync.dma_start(out=planes[i][0:P:8, :].bitcast(I32), in_=src[0].bitcast(I32))
+        nc.sync.dma_start(out=words[0][:], in_=tab_words[0].rearrange("p t i -> p (t i)").bitcast(I32))
         for i, src in enumerate((wer_scales, wei_scales, wrr_scales, wri_scales)):
-            nc.gpsimd.dma_start(out=s_raw[0:P:8, i, :], in_=src[0].bitcast(I32))
+            nc.sync.dma_start(out=s_raw[0:P:8, i, :], in_=src[0].bitcast(I32))
+        nc.sync.dma_start(out=w_raw[:, 3, :], in_=w_src[3][0].bitcast(I32))
+        nc.sync.dma_start(out=words[1][:], in_=tab2_words[0].rearrange("p t i -> p (t i)").bitcast(I32))
 
         g_words = {}
-        g_plane = keep.tile([P, 2 * J], U8, name="g_plane", align_bytes=64)
+        g_plane = big.tile([P, 2 * J], U8, name="g_plane", align_bytes=64, offset=10 * T + 4 * R)
 
         def gather_words(i, h):
             cols = HALF // 16
             g_words[i, h] = big.tile([P, HALF], U32, name=f"g_words{i}{h}", align_bytes=64,
-                                     offset=8 * T + T * (1 - i) + 4 * HALF * h)
+                                     offset=G_AT[i][h])
             nc.vector.tensor_copy(g_words[i, h][:], words[i][:].bitcast(U32).indirect(lists[i][:, h * cols : (h + 1) * cols]))
 
         for i in range(2):
@@ -134,16 +137,24 @@ def tile_list_ckg_none_kernel(tc, tab_words, tab_scales, tab2_words, tab2_scales
             jj = jt - GROUPS[g][0]
             if jj == 0:
                 h_bf[g] = ring.tile([P, 2, len(GROUPS[g]) * P, PACK], BF16, name="h_bf", align_bytes=64, bufs=3)
-            engine = nc.vector if jt == TILES - 1 else nc.gpsimd
-            engine.tensor_tensor(h_bf[g][:, :, jj * P : (jj + 1) * P, :], prods[jt][0][:], prods[jt][1][:], ADD)
+            if jt < TILES - 1:
+                nc.gpsimd.tensor_tensor(h_bf[g][:, :, jj * P : (jj + 1) * P, :], prods[jt][0][:], prods[jt][1][:], ADD)
+            else:
+                for c in range(2):
+                    nc.vector.tensor_tensor(h_bf[g][:, c], prods[jt][0][:, c], prods[jt][1][:, c], ADD)
 
         def quantise(g):
             W = len(GROUPS[g]) * P
             codes = ring.tile([P, 2, W], U32, name="h_codes", align_bytes=64)
             plane = ring.tile([P, 2, W], U8, name="h_plane", align_bytes=64)
-            nc.vector.quantize_mx(out=codes[:].rearrange("p c j -> p (c j)").bitcast(FP8X4),
-                                  scales=plane[:].rearrange("p c j -> p (c j)"),
-                                  in_=h_bf[g][:].rearrange("p c j t -> p (c j t)"))
+            if g < len(GROUPS) - 1:
+                nc.vector.quantize_mx(out=codes[:].rearrange("p c j -> p (c j)").bitcast(FP8X4),
+                                      scales=plane[:].rearrange("p c j -> p (c j)"),
+                                      in_=h_bf[g][:].rearrange("p c j t -> p (c j t)"))
+            else:
+                for c in range(2):
+                    nc.vector.quantize_mx(out=codes[:, c, :].bitcast(FP8X4), scales=plane[:, c, :],
+                                          in_=h_bf[g][:, c].rearrange("p j t -> p (j t)"))
             h_q[g] = (codes, plane)
 
         def score(g):
@@ -164,7 +175,7 @@ def tile_list_ckg_none_kernel(tc, tab_words, tab_scales, tab2_words, tab2_scales
         for jt in range(AHEAD):
             entity(jt)
         relation(0)
-        for jt in range(TILES + 2):
+        for jt in range(TILES):
             if jt < TILES:
                 products(jt)
             if jt + 1 < TILES:
@@ -177,9 +188,12 @@ def tile_list_ckg_none_kernel(tc, tab_words, tab_scales, tab2_words, tab2_scales
             if jt == 3:
                 nc.vector.quantize_mx(out=n_codes[:].bitcast(FP8X4), scales=n_plane[:],
                                       in_=n_bf[:].rearrange("p c n t -> p (c n t)"))
-            if jt < TILES:
+            if jt < TILES - 1:
                 turn(jt)
-            for g in range(len(GROUPS)):
-                if min(GROUPS[g][-1] + 2, TILES) == jt:
+            for g in range(len(GROUPS) - 1):
+                if min(GROUPS[g][-1] + 2, TILES - 1) == jt:
                     quantise(g)
                     score(g)
+        turn(TILES - 1)
+        quantise(len(GROUPS) - 1)
+        score(len(GROUPS) - 1)

@@ -1,6 +1,7 @@
 from contextlib import ExitStack
 
 import concourse.mybir as mybir
+from concourse.masks import make_identity
 
 K, L, R, N, T, J = 512, 512, 512, 256, 4096, 1024
 FLOPS = 2 * 4 * K * R * J + 2 * 2 * R * N * J
@@ -22,7 +23,9 @@ HALF = J // 2
 TILES = J // P
 AHEAD = 2
 G_AT = ((10 * T + 2 * R, 11 * T), (8 * T, 9 * T))
+TURNED = (3, 6)
 GROUPS = ((0, 1), (2, 3), (4, 5), (6,), (7,))
+QUANTISE_IN = {4: (0,), 7: (1, 2)}
 GROUP_OF = {jt: g for g, tiles in enumerate(GROUPS) for jt in tiles}
 
 
@@ -46,6 +49,8 @@ def tile_list_ckg_none_kernel(tc, tab_words, tab_scales, tab2_words, tab2_scales
         nc.vector.memset(planes[0][:].bitcast(I32), 0)
         nc.gpsimd.memset(planes[1][:].bitcast(I32), 0)
         nc.vector.memset(s_raw[:], 0)
+        ident = keep.tile([P, P], F32, name="ident")
+        make_identity(nc, ident[:])
 
         w_src = (wer_words, wei_words, wrr_words, wri_words)
         nc.sync.dma_start(lists[0][:], offs)
@@ -94,13 +99,21 @@ def tile_list_ckg_none_kernel(tc, tab_words, tab_scales, tab2_words, tab2_scales
         def project(tab, w, jt, bank):
             h, c = divmod(jt * P, HALF)
             s0 = 4 * R + tab * J + jt * P
+            if jt in TURNED:
+                nc.tensor.matmul_mx(out=bank[:].rearrange("j t p -> j (t p)"),
+                                    lhsT=g_words[tab, h][:, c : c + P].bitcast(FP8X4), lhsT_scale=plane_all[:, s0 : s0 + P],
+                                    rhs=w_words[:, w].rearrange("p t m -> p (t m)").bitcast(U8).bitcast(FP4X4),
+                                    rhs_scale=plane_all[:, w * R : (w + 1) * R], start=True, stop=True)
+                return
             for t in range(PACK):
                 nc.tensor.matmul_mx(out=bank[:, t, :], lhsT=w_words[:, w, t, :].bitcast(U8).bitcast(FP4X4),
                                     lhsT_scale=plane_all[:, w * R + t * P : w * R + (t + 1) * P],
                                     rhs=g_words[tab, h][:, c : c + P].bitcast(FP8X4), rhs_scale=plane_all[:, s0 : s0 + P],
                                     start=True, stop=True)
 
-        def woven(bank):
+        def stream(jt, bank):
+            if jt in TURNED:
+                return bank[:].rearrange("j t p -> j (t p)").rearrange("j (a b) -> j a b", b=PACK)
             return bank[:].rearrange("p t j -> p j t")
 
         ent = {}
@@ -112,9 +125,9 @@ def tile_list_ckg_none_kernel(tc, tab_words, tab_scales, tab2_words, tab2_scales
         def entity(jt):
             ent[jt] = ring.tile([P, 2, P, PACK], F32, name="ent", bufs=AHEAD + 1)
             for c in range(2):
-                bank = psum.tile([P, PACK, P], F32, name="e_bank", bufs=2)
+                bank = psum.tile([P, PACK, P], F32, name="e_bank", tag="e_bank", bufs=2)
                 project(0, c, jt, bank)
-                nc.scalar.copy(ent[jt][:, c], woven(bank))
+                nc.scalar.copy(ent[jt][:, c], stream(jt, bank))
 
         def relation(jt):
             rel[jt] = []
@@ -123,25 +136,43 @@ def tile_list_ckg_none_kernel(tc, tab_words, tab_scales, tab2_words, tab2_scales
                 project(1, 2 + c, jt, bank)
                 rel[jt].append(bank)
 
-        def products(jt):
+        def products_arr(jt):
             pa = ring.tile([P, 2, P, PACK], F32, name="pa", bufs=3)
-            pb = ring.tile([P, 2, P, PACK], F32, name="pb", bufs=3)
-            arr, ari = woven(rel[jt][0]), woven(rel[jt][1])
+            arr = stream(jt, rel[jt][0])
             nc.vector.tensor_tensor(pa[:], arr.unsqueeze(1).to_broadcast([P, 2, P, PACK]), ent[jt][:], MULT)
+            prods[jt] = [pa]
+
+        def products_ari_negated(jt):
+            pb = ring.tile([P, 2, P, PACK], F32, name="pb", bufs=3)
+            ari = stream(jt, rel[jt][1])
             nc.vector.scalar_tensor_tensor(pb[:, 0], ari, -1.0, ent[jt][:, 1], MULT, MULT)
-            nc.vector.tensor_tensor(pb[:, 1], ari, ent[jt][:, 0], MULT)
-            prods[jt] = (pa, pb)
+            prods[jt].append(pb)
+
+        def products_ari(jt):
+            nc.vector.tensor_tensor(prods[jt][1][:, 1], stream(jt, rel[jt][1]), ent[jt][:, 0], MULT)
 
         def turn(jt):
             g = GROUP_OF[jt]
             jj = jt - GROUPS[g][0]
             if jj == 0:
-                h_bf[g] = ring.tile([P, 2, len(GROUPS[g]) * P, PACK], BF16, name="h_bf", align_bytes=64, bufs=3)
-            if jt < TILES - 1:
-                nc.gpsimd.tensor_tensor(h_bf[g][:, :, jj * P : (jj + 1) * P, :], prods[jt][0][:], prods[jt][1][:], ADD)
-            else:
+                h_bf[g] = ring.tile([P, 2, len(GROUPS[g]) * P, PACK], BF16, name="h_bf", align_bytes=64, bufs=4)
+            dst = h_bf[g][:, :, jj * P : (jj + 1) * P, :]
+            if jt == TILES - 1:
                 for c in range(2):
-                    nc.vector.tensor_tensor(h_bf[g][:, c], prods[jt][0][:, c], prods[jt][1][:, c], ADD)
+                    nc.vector.tensor_tensor(dst[:, c], prods[jt][0][:, c], prods[jt][1][:, c], ADD)
+                return
+            if jt not in TURNED:
+                nc.gpsimd.tensor_tensor(dst, prods[jt][0][:], prods[jt][1][:], ADD)
+                return
+            banks = [psum.tile([P, PACK, P], F32, name="h_bank", tag="hy", bufs=2) for c in range(2)]
+            for s in range(2):
+                for c in range(2):
+                    src = prods[jt][s][:, c].rearrange("j a b -> j (a b)")
+                    for t in range(PACK):
+                        nc.tensor.matmul(banks[c][:, t, :], src[:, t * P : (t + 1) * P], ident[:], is_transpose=True,
+                                         start=(s == 0 and t == 0), stop=(s == 1 and t == PACK - 1))
+            for c in range(2):
+                nc.scalar.copy(dst[:, c], banks[c][:].rearrange("p t j -> p j t"))
 
         def quantise(g):
             W = len(GROUPS[g]) * P
@@ -161,7 +192,7 @@ def tile_list_ckg_none_kernel(tc, tab_words, tab_scales, tab2_words, tab2_scales
             codes, plane = h_q[g]
             W = len(GROUPS[g]) * P
             j0 = GROUPS[g][0] * P
-            bank = psum.tile([P, 2, W], F32, name="y_bank", bufs=2)
+            bank = psum.tile([P, 2, W], F32, name="y_bank", tag="e_bank", bufs=2)
             for c in range(2):
                 for nt in range(2):
                     cols = slice(c * N + nt * P, c * N + (nt + 1) * P)
@@ -174,26 +205,26 @@ def tile_list_ckg_none_kernel(tc, tab_words, tab_scales, tab2_words, tab2_scales
 
         for jt in range(AHEAD):
             entity(jt)
-        relation(0)
+            relation(jt)
         for jt in range(TILES):
-            if jt < TILES:
-                products(jt)
-            if jt + 1 < TILES:
-                relation(jt + 1)
-            if jt + AHEAD < TILES:
-                entity(jt + AHEAD)
-            if jt == 1:
-                for c in range(2):
-                    nc.scalar.copy(n_bf[:, c], n_raw[c][:].rearrange("p t n -> p n t"))
-            if jt == 3:
+            products_arr(jt)
+            products_ari_negated(jt)
+            if jt == 4:
                 nc.vector.quantize_mx(out=n_codes[:].bitcast(FP8X4), scales=n_plane[:],
                                       in_=n_bf[:].rearrange("p c n t -> p (c n t)"))
-            if jt < TILES - 1:
-                turn(jt)
-            for g in range(len(GROUPS) - 1):
-                if min(GROUPS[g][-1] + 2, TILES - 1) == jt:
-                    quantise(g)
-                    score(g)
-        turn(TILES - 1)
-        quantise(len(GROUPS) - 1)
-        score(len(GROUPS) - 1)
+            for g in QUANTISE_IN.get(jt, ()):
+                quantise(g)
+            products_ari(jt)
+            if jt + AHEAD < TILES:
+                relation(jt + AHEAD)
+                entity(jt + AHEAD)
+            if jt in (1, 2):
+                for h in range(2):
+                    cols = slice(h * P, (h + 1) * P)
+                    nc.scalar.copy(n_bf[:, jt - 1, cols, :], n_raw[jt - 1][:, :, cols].rearrange("p t n -> p n t"))
+            turn(jt)
+            for g in QUANTISE_IN.get(jt, ()):
+                score(g)
+        for g in (3, 4):
+            quantise(g)
+            score(g)

@@ -85,6 +85,11 @@ def tile_list_ckg_none_kernel(tc, tab_words, tab_scales, tab2_words, tab2_scales
                               w_raw[:].rearrange("p w (m t k) -> p w t m k", t=PACK, k=2))
         gather_words(0, 0)
         gather_words(0, 1)
+        warm = psum.tile([P, HALF], F32, name="warm", tag="hy", bufs=2)
+        for h in range(2):
+            for rep in range(2):
+                nc.tensor.matmul_mx(out=warm[:], lhsT=g_words[0, h][:, rep * P : (rep + 1) * P].bitcast(FP8X4), lhsT_scale=planes[1][:, 0:P],
+                                    rhs=w_words[:, rep].rearrange("p t m -> p (t m)").bitcast(U8).bitcast(FP4X4), rhs_scale=planes[1][:, 0:R], start=True, stop=True)
         n_raw = [big.tile([P, PACK, N], F32, name=f"n_raw{i}", align_bytes=64, offset=16 * N * i) for i in range(2)]
         for c, src in enumerate((nr, ni)):
             for i in range(4):

@@ -127,34 +127,35 @@ def tile_list_ckg_none_kernel(tc, tab_words, tab_scales, tab2_words, tab2_scales
         h_bf = {}
         h_q = {}
 
-        def entity(jt):
-            ent[jt] = ring.tile([P, 2, P, PACK], F32, name="ent", bufs=AHEAD + 1)
-            for c in range(2):
-                bank = psum.tile([P, PACK, P], F32, name="e_bank", tag="e_bank", bufs=2)
-                project(0, c, jt, bank)
-                nc.scalar.copy(ent[jt][:, c], stream(jt, bank))
+        def entity(jt, c):
+            if c == 0:
+                ent[jt] = ring.tile([P, 2, P, PACK], F32, name="ent", bufs=AHEAD + 1)
+            bank = psum.tile([P, PACK, P], F32, name="e_bank", tag="e_bank", bufs=2)
+            project(0, c, jt, bank)
+            nc.scalar.copy(ent[jt][:, c], stream(jt, bank))
 
-        def relation(jt):
-            rel[jt] = []
-            for c in range(2):
-                bank = psum.tile([P, PACK, P], F32, name="r_bank", bufs=4)
-                project(1, 2 + c, jt, bank)
-                rel[jt].append(bank)
+        def relation(jt, c):
+            rel[jt, c] = psum.tile([P, PACK, P], F32, name="r_bank", bufs=4)
+            project(1, 2 + c, jt, rel[jt, c])
 
         def products_arr(jt):
             pa = ring.tile([P, 2, P, PACK], F32, name="pa", bufs=3)
-            arr = stream(jt, rel[jt][0])
-            nc.vector.tensor_tensor(pa[:], arr.unsqueeze(1).to_broadcast([P, 2, P, PACK]), ent[jt][:], MULT)
+            arr = stream(jt, rel[jt, 0])
+            if jt == 0:
+                for c in range(2):
+                    nc.vector.tensor_tensor(pa[:, c], arr, ent[jt][:, c], MULT)
+            else:
+                nc.vector.tensor_tensor(pa[:], arr.unsqueeze(1).to_broadcast([P, 2, P, PACK]), ent[jt][:], MULT)
             prods[jt] = [pa]
 
         def products_ari_negated(jt):
             pb = ring.tile([P, 2, P, PACK], F32, name="pb", bufs=3)
-            ari = stream(jt, rel[jt][1])
+            ari = stream(jt, rel[jt, 1])
             nc.vector.scalar_tensor_tensor(pb[:, 0], ari, -1.0, ent[jt][:, 1], MULT, MULT)
             prods[jt].append(pb)
 
         def products_ari(jt):
-            nc.vector.tensor_tensor(prods[jt][1][:, 1], stream(jt, rel[jt][1]), ent[jt][:, 0], MULT)
+            nc.vector.tensor_tensor(prods[jt][1][:, 1], stream(jt, rel[jt, 1]), ent[jt][:, 0], MULT)
 
         def turn(jt):
             g = GROUP_OF[jt]
@@ -209,8 +210,9 @@ def tile_list_ckg_none_kernel(tc, tab_words, tab_scales, tab2_words, tab2_scales
             nc.sync.dma_start(out=out.rearrange("(nt p) j -> p nt j", p=P)[:, :, j0 : j0 + W], in_=y[:])
 
         for jt in range(AHEAD):
-            entity(jt)
-            relation(jt)
+            for c in range(2):
+                entity(jt, c)
+                relation(jt, c)
         for jt in range(TILES):
             products_arr(jt)
             products_ari_negated(jt)
@@ -221,8 +223,9 @@ def tile_list_ckg_none_kernel(tc, tab_words, tab_scales, tab2_words, tab2_scales
                 quantise(g)
             products_ari(jt)
             if jt + AHEAD < TILES:
-                relation(jt + AHEAD)
-                entity(jt + AHEAD)
+                for stage in (relation, entity):
+                    for c in range(2):
+                        stage(jt + AHEAD, c)
             if jt in (1, 2):
                 for h in range(2):
                     cols = slice(h * P, (h + 1) * P)

@@ -22,7 +22,10 @@ PACK = 4
 HALF = J // 2
 TILES = J // P
 AHEAD = 2
-G_AT = ((10 * T + 2 * R, 11 * T), (8 * T, 9 * T))
+LEAD = T // 8
+S_AT = 14 * T
+G_AT = ((10 * T - 3 * R, 10 * T + 3 * R), (12 * T, 13 * T))
+W_AT = (10 * T + R, S_AT)
 TURNED = (3, 6)
 GROUPS = ((0, 1), (2, 3), (4, 5), (6,), (7,))
 QUANTISE_IN = {4: (0,), 7: (1, 2)}
@@ -40,14 +43,13 @@ def tile_list_ckg_none_kernel(tc, tab_words, tab_scales, tab2_words, tab2_scales
 
         lists = [keep.tile([P, J // 16], U16, name=f"list{i}") for i in range(2)]
         words = [big.tile([P, T], I32, name=f"words{i}", align_bytes=64, offset=4 * T * i) for i in range(2)]
-        planes = [big.tile([P, T], U8, name=f"plane{i}", align_bytes=64, offset=8 * T + T * i) for i in range(2)]
-        w_raw = big.tile([P, 4, R // 2], I32, name="w_raw", align_bytes=64, offset=11 * T)
-        w_words = keep.tile([P, 4, PACK, P // 2], I32, name="w_words", align_bytes=64)
-        s_raw = big.tile([P, 4, R // 4], I32, name="s_raw", align_bytes=64, offset=10 * T)
+        planes = [big.tile([P, T], U8, name=f"plane{i}", align_bytes=64, offset=16 * T + T * i) for i in range(2)]
+        w_words = {}
+        s_raw = big.tile([P, 4, R // 4], I32, name="s_raw", align_bytes=64, offset=S_AT)
         plane_all = keep.tile([P, 4 * R + 2 * J], U8, name="plane_all", align_bytes=64)
 
-        nc.vector.memset(planes[0][:].bitcast(I32), 0)
-        nc.gpsimd.memset(planes[1][:].bitcast(I32), 0)
+        nc.gpsimd.memset(planes[0][:].bitcast(I32), 0)
+        nc.vector.memset(planes[1][:].bitcast(I32), 0)
         nc.vector.memset(s_raw[:], 0)
         ident = keep.tile([P, P], F32, name="ident")
         make_identity(nc, ident[:])
@@ -55,18 +57,21 @@ def tile_list_ckg_none_kernel(tc, tab_words, tab_scales, tab2_words, tab2_scales
         w_src = (wer_words, wei_words, wrr_words, wri_words)
         nc.sync.dma_start(lists[0][:], offs)
         nc.sync.dma_start(lists[1][:], offs2)
-        for i in range(3):
-            nc.sync.dma_start(out=w_raw[:, i, :], in_=w_src[i][0].bitcast(I32))
+        w_raw = {}
+        for w in range(2):
+            w_raw[w] = big.tile([P, R // 2], I32, name=f"w_raw{w}", align_bytes=64, offset=15 * T + 2 * R * w)
+            nc.sync.dma_start(out=w_raw[w][:], in_=w_src[w][0].bitcast(I32))
+        tab = tab_words[0].rearrange("p t i -> p (t i)").bitcast(I32)
+        nc.sync.dma_start(out=words[0][:, :LEAD], in_=tab[:, :LEAD])
         for i, src in enumerate((tab_scales, tab2_scales)):
             nc.sync.dma_start(out=planes[i][0:P:8, :].bitcast(I32), in_=src[0].bitcast(I32))
-        nc.sync.dma_start(out=words[0][:], in_=tab_words[0].rearrange("p t i -> p (t i)").bitcast(I32))
+        nc.sync.dma_start(out=words[0][:, LEAD:], in_=tab[:, LEAD:])
         for i, src in enumerate((wer_scales, wei_scales, wrr_scales, wri_scales)):
             nc.sync.dma_start(out=s_raw[0:P:8, i, :], in_=src[0].bitcast(I32))
-        nc.sync.dma_start(out=w_raw[:, 3, :], in_=w_src[3][0].bitcast(I32))
         nc.sync.dma_start(out=words[1][:], in_=tab2_words[0].rearrange("p t i -> p (t i)").bitcast(I32))
 
         g_words = {}
-        g_plane = big.tile([P, 2 * J], U8, name="g_plane", align_bytes=64, offset=10 * T + 4 * R)
+        g_plane = big.tile([P, 2 * J], U8, name="g_plane", align_bytes=64, offset=10 * T)
 
         def gather_words(i, h):
             cols = HALF // 16
@@ -76,26 +81,36 @@ def tile_list_ckg_none_kernel(tc, tab_words, tab_scales, tab2_words, tab2_scales
 
         for i in range(2):
             nc.vector.tensor_copy(g_plane[:, i * J : (i + 1) * J], planes[i][:].indirect(lists[i][:]))
-        nc.vector.tensor_copy(plane_all[:, 0 : 4 * R].bitcast(I32).rearrange("p (w t m) -> p w t m", w=4, t=PACK),
+        nc.gpsimd.tensor_copy(plane_all[:, 0 : 4 * R].bitcast(I32).rearrange("p (w t m) -> p w t m", w=4, t=PACK),
                               s_raw[:].rearrange("p w (m t) -> p w t m", t=PACK))
         nc.vector.tensor_copy(plane_all[:, 4 * R :].bitcast(I32), g_plane[:].bitcast(I32))
         for r in range(1, 4):
-            nc.scalar.dma_start(out=plane_all[r:P:32, :].bitcast(I32), in_=plane_all[8 * r : P : 32, :].bitcast(I32))
-        nc.vector.tensor_copy(w_words[:].rearrange("p w t (m k) -> p w t m k", k=2),
-                              w_raw[:].rearrange("p w (m t k) -> p w t m k", t=PACK, k=2))
+            nc.sync.dma_start(out=plane_all[r:P:32, :].bitcast(I32), in_=plane_all[8 * r : P : 32, :].bitcast(I32))
+        for i, w in enumerate((2, 3)):
+            w_raw[w] = big.tile([P, R // 2], I32, name=f"w_raw{w}", align_bytes=64, offset=W_AT[i])
+            nc.sync.dma_start(out=w_raw[w][:], in_=w_src[w][0].bitcast(I32))
+
+        def deal(w):
+            w_words[w] = keep.tile([P, PACK, P // 2], I32, name=f"w_words{w}", align_bytes=64)
+            (nc.vector if w < 2 else nc.gpsimd).tensor_copy(w_words[w][:].rearrange("p t (m k) -> p t m k", k=2),
+                                  w_raw[w][:].rearrange("p (m t k) -> p t m k", t=PACK, k=2))
+
+        deal(0)
+        deal(1)
         gather_words(0, 0)
         gather_words(0, 1)
         warm = psum.tile([P, HALF], F32, name="warm", tag="hy", bufs=2)
-        for h in range(2):
-            for rep in range(2):
-                nc.tensor.matmul_mx(out=warm[:], lhsT=g_words[0, h][:, rep * P : (rep + 1) * P].bitcast(FP8X4), lhsT_scale=planes[1][:, 0:P],
-                                    rhs=w_words[:, rep].rearrange("p t m -> p (t m)").bitcast(U8).bitcast(FP4X4), rhs_scale=planes[1][:, 0:R], start=True, stop=True)
+        for rep in range(4):
+                nc.tensor.matmul_mx(out=warm[:], lhsT=g_words[0, 0][:, rep * P : (rep + 1) * P].bitcast(FP8X4), lhsT_scale=planes[0][:, 0:P],
+                                    rhs=w_words[0][:].rearrange("p t m -> p (t m)").bitcast(U8).bitcast(FP4X4), rhs_scale=planes[0][:, 0:R], start=True, stop=True)
+        gather_words(1, 0)
+        deal(2)
+        gather_words(1, 1)
+        deal(3)
         n_raw = [big.tile([P, PACK, N], F32, name=f"n_raw{i}", align_bytes=64, offset=16 * N * i) for i in range(2)]
         for c, src in enumerate((nr, ni)):
             for i in range(4):
                 nc.sync.dma_start(out=n_raw[c][i:P:4], in_=src.rearrange("(m t i) n -> i m t n", t=PACK, i=4)[i])
-        gather_words(1, 0)
-        gather_words(1, 1)
 
         n_bf = keep.tile([P, 2, N, PACK], BF16, name="n_bf", align_bytes=64)
         n_codes = keep.tile([P, 2 * N], U32, name="n_codes", align_bytes=64)
@@ -107,11 +122,11 @@ def tile_list_ckg_none_kernel(tc, tab_words, tab_scales, tab2_words, tab2_scales
             if jt in TURNED:
                 nc.tensor.matmul_mx(out=bank[:].rearrange("j t p -> j (t p)"),
                                     lhsT=g_words[tab, h][:, c : c + P].bitcast(FP8X4), lhsT_scale=plane_all[:, s0 : s0 + P],
-                                    rhs=w_words[:, w].rearrange("p t m -> p (t m)").bitcast(U8).bitcast(FP4X4),
+                                    rhs=w_words[w][:].rearrange("p t m -> p (t m)").bitcast(U8).bitcast(FP4X4),
                                     rhs_scale=plane_all[:, w * R : (w + 1) * R], start=True, stop=True)
                 return
             for t in range(PACK):
-                nc.tensor.matmul_mx(out=bank[:, t, :], lhsT=w_words[:, w, t, :].bitcast(U8).bitcast(FP4X4),
+                nc.tensor.matmul_mx(out=bank[:, t, :], lhsT=w_words[w][:, t, :].bitcast(U8).bitcast(FP4X4),
                                     lhsT_scale=plane_all[:, w * R + t * P : w * R + (t + 1) * P],
                                     rhs=g_words[tab, h][:, c : c + P].bitcast(FP8X4), rhs_scale=plane_all[:, s0 : s0 + P],
                                     start=True, stop=True)

@@ -22,13 +22,18 @@ PACK = 4
 HALF = J // 2
 TILES = J // P
 AHEAD = 2
+SLOT = 4096
+PA_AT, PB_AT = 18 * T, 26 * T
+N_AT, ARR_AT, H_AT = 34 * T, 36 * T, 38 * T
+CODES_AT = (ARR_AT - SLOT // 4, N_AT, PB_AT + 5 * SLOT, PA_AT, PB_AT)
 LEAD = T // 8
 S_AT = 14 * T
 G_AT = ((10 * T - 3 * R, 10 * T + 3 * R), (12 * T, 13 * T))
 W_AT = (10 * T + R, S_AT)
 TURNED = (3, 6)
 GROUPS = ((0, 1), (2, 3), (4, 5), (6,), (7,))
-QUANTISE_IN = {4: (0,), 7: (1, 2)}
+SHARED = 3
+QUANTISE_IN = {5: (0, 1), 7: (2,)}
 GROUP_OF = {jt: g for g, tiles in enumerate(GROUPS) for jt in tiles}
 
 
@@ -112,8 +117,7 @@ def tile_list_ckg_none_kernel(tc, tab_words, tab_scales, tab2_words, tab2_scales
             for i in range(4):
                 nc.sync.dma_start(out=n_raw[c][i:P:4], in_=src.rearrange("(m t i) n -> i m t n", t=PACK, i=4)[i])
 
-        n_bf = keep.tile([P, 2, N, PACK], BF16, name="n_bf", align_bytes=64)
-        n_codes = keep.tile([P, 2 * N], U32, name="n_codes", align_bytes=64)
+        n_bf = big.tile([P, 2, N, PACK], BF16, name="n_bf", align_bytes=64, offset=N_AT)
         n_plane = keep.tile([P, 2 * N], U8, name="n_plane", align_bytes=64)
 
         def project(tab, w, jt, bank):
@@ -144,7 +148,7 @@ def tile_list_ckg_none_kernel(tc, tab_words, tab_scales, tab2_words, tab2_scales
 
         def entity(jt, c):
             if c == 0:
-                ent[jt] = ring.tile([P, 2, P, PACK], F32, name="ent", bufs=AHEAD + 1)
+                ent[jt] = ring.tile([P, 2, P, PACK], F32, name="ent", bufs=AHEAD + 2)
             bank = psum.tile([P, PACK, P], F32, name="e_bank", tag="e_bank", bufs=2)
             project(0, c, jt, bank)
             nc.scalar.copy(ent[jt][:, c], stream(jt, bank))
@@ -152,9 +156,17 @@ def tile_list_ckg_none_kernel(tc, tab_words, tab_scales, tab2_words, tab2_scales
         def relation(jt, c):
             rel[jt, c] = psum.tile([P, PACK, P], F32, name="r_bank", bufs=4)
             project(1, 2 + c, jt, rel[jt, c])
+            if (jt, c) == (SHARED, 0):
+                arr = big.tile([P, P, PACK], F32, name="arr", align_bytes=64, offset=ARR_AT)
+                nc.scalar.copy(arr[:], stream(jt, rel[jt, c]))
+                pa = big.tile([P, 2, P, PACK], F32, name=f"pa{jt}", offset=PA_AT + SLOT * jt)
+                nc.gpsimd.tensor_tensor(pa[:], arr[:].unsqueeze(1).to_broadcast([P, 2, P, PACK]), ent[jt][:], MULT)
+                prods[jt] = [pa]
 
         def products_arr(jt):
-            pa = ring.tile([P, 2, P, PACK], F32, name="pa", bufs=3)
+            if jt == SHARED:
+                return
+            pa = big.tile([P, 2, P, PACK], F32, name=f"pa{jt}", offset=ARR_AT - SLOT if jt == 2 else PA_AT + SLOT * jt)
             arr = stream(jt, rel[jt, 0])
             if jt == 0:
                 for c in range(2):
@@ -164,7 +176,7 @@ def tile_list_ckg_none_kernel(tc, tab_words, tab_scales, tab2_words, tab2_scales
             prods[jt] = [pa]
 
         def products_ari_negated(jt):
-            pb = ring.tile([P, 2, P, PACK], F32, name="pb", bufs=3)
+            pb = big.tile([P, 2, P, PACK], F32, name=f"pb{jt}", offset=ARR_AT + SLOT // 2 if jt == 2 else PB_AT + SLOT * jt)
             ari = stream(jt, rel[jt, 1])
             nc.vector.scalar_tensor_tensor(pb[:, 0], ari, -1.0, ent[jt][:, 1], MULT, MULT)
             prods[jt].append(pb)
@@ -176,7 +188,8 @@ def tile_list_ckg_none_kernel(tc, tab_words, tab_scales, tab2_words, tab2_scales
             g = GROUP_OF[jt]
             jj = jt - GROUPS[g][0]
             if jj == 0:
-                h_bf[g] = ring.tile([P, 2, len(GROUPS[g]) * P, PACK], BF16, name="h_bf", align_bytes=64, bufs=4)
+                h_bf[g] = big.tile([P, 2, len(GROUPS[g]) * P, PACK], BF16, name=f"h_bf{g}", align_bytes=64,
+                                   offset=H_AT + SLOT * (0, 1, 1, 3, 1)[g])
             dst = h_bf[g][:, :, jj * P : (jj + 1) * P, :]
             if jt == TILES - 1:
                 for c in range(2):
@@ -197,8 +210,8 @@ def tile_list_ckg_none_kernel(tc, tab_words, tab_scales, tab2_words, tab2_scales
 
         def quantise(g):
             W = len(GROUPS[g]) * P
-            codes = ring.tile([P, 2, W], U32, name="h_codes", align_bytes=64)
-            plane = ring.tile([P, 2, W], U8, name="h_plane", align_bytes=64)
+            codes = big.tile([P, 2, W], U32, name=f"h_codes{g}", align_bytes=64, offset=CODES_AT[g])
+            plane = keep.tile([P, 2, W], U8, name=f"h_plane{g}", align_bytes=64)
             if g < len(GROUPS) - 1:
                 nc.vector.quantize_mx(out=codes[:].rearrange("p c j -> p (c j)").bitcast(FP8X4),
                                       scales=plane[:].rearrange("p c j -> p (c j)"),
@@ -231,21 +244,27 @@ def tile_list_ckg_none_kernel(tc, tab_words, tab_scales, tab2_words, tab2_scales
         for jt in range(TILES):
             products_arr(jt)
             products_ari_negated(jt)
-            if jt == 4:
+            if jt == 5:
+                n_codes = big.tile([P, 2 * N], U32, name="n_codes", align_bytes=64, offset=ARR_AT + SLOT // 4)
                 nc.vector.quantize_mx(out=n_codes[:].bitcast(FP8X4), scales=n_plane[:],
                                       in_=n_bf[:].rearrange("p c n t -> p (c n t)"))
-            for g in QUANTISE_IN.get(jt, ()):
-                quantise(g)
+                quantise(0)
+                quantise(1)
+                turn(4)
             products_ari(jt)
+            if jt == 7:
+                for g in QUANTISE_IN[jt]:
+                    quantise(g)
             if jt + AHEAD < TILES:
-                for stage in (relation, entity):
+                for stage in ((entity, relation) if jt + AHEAD == SHARED else (relation, entity)):
                     for c in range(2):
                         stage(jt + AHEAD, c)
             if jt in (1, 2):
                 for h in range(2):
                     cols = slice(h * P, (h + 1) * P)
                     nc.scalar.copy(n_bf[:, jt - 1, cols, :], n_raw[jt - 1][:, :, cols].rearrange("p t n -> p n t"))
-            turn(jt)
+            if jt != 4:
+                turn(jt)
             for g in QUANTISE_IN.get(jt, ()):
                 score(g)
         for g in (3, 4):

@@ -25,15 +25,16 @@ AHEAD = 2
 SLOT = 4096
 PA_AT, PB_AT = 18 * T, 26 * T
 N_AT, ARR_AT, H_AT = 34 * T, 36 * T, 38 * T
-CODES_AT = (ARR_AT - SLOT // 4, N_AT, PB_AT + 5 * SLOT, PA_AT, PB_AT)
+CODES_AT = (ARR_AT - SLOT // 4, N_AT, PB_AT + 5 * SLOT, PA_AT + 5 * SLOT, PB_AT)
 LEAD = T // 8
-S_AT = 14 * T
+S_AT = 46 * T
 G_AT = ((10 * T - 3 * R, 10 * T + 3 * R), (12 * T, 13 * T))
-W_AT = (10 * T + R, S_AT)
+W_AT = (10 * T + R, S_AT + R)
+NR_AT = (S_AT + R - 16 * N, S_AT + 3 * R)
 TURNED = (3, 6)
 GROUPS = ((0, 1), (2, 3), (4, 5), (6,), (7,))
 SHARED = 3
-QUANTISE_IN = {5: (0, 1), 7: (2,)}
+HALVED = (0, 1)
 GROUP_OF = {jt: g for g, tiles in enumerate(GROUPS) for jt in tiles}
 
 
@@ -112,7 +113,7 @@ def tile_list_ckg_none_kernel(tc, tab_words, tab_scales, tab2_words, tab2_scales
         deal(2)
         gather_words(1, 1)
         deal(3)
-        n_raw = [big.tile([P, PACK, N], F32, name=f"n_raw{i}", align_bytes=64, offset=16 * N * i) for i in range(2)]
+        n_raw = [big.tile([P, PACK, N], F32, name=f"n_raw{i}", align_bytes=64, offset=NR_AT[i]) for i in range(2)]
         for c, src in enumerate((nr, ni)):
             for i in range(4):
                 nc.sync.dma_start(out=n_raw[c][i:P:4], in_=src.rearrange("(m t i) n -> i m t n", t=PACK, i=4)[i])
@@ -154,7 +155,7 @@ def tile_list_ckg_none_kernel(tc, tab_words, tab_scales, tab2_words, tab2_scales
             nc.scalar.copy(ent[jt][:, c], stream(jt, bank))
 
         def relation(jt, c):
-            rel[jt, c] = psum.tile([P, PACK, P], F32, name="r_bank", bufs=4)
+            rel[jt, c] = psum.tile([P, PACK, P], F32, name="r_bank", tag="r_bank", bufs=4)
             project(1, 2 + c, jt, rel[jt, c])
             if (jt, c) == (SHARED, 0):
                 arr = big.tile([P, P, PACK], F32, name="arr", align_bytes=64, offset=ARR_AT)
@@ -168,9 +169,8 @@ def tile_list_ckg_none_kernel(tc, tab_words, tab_scales, tab2_words, tab2_scales
                 return
             pa = big.tile([P, 2, P, PACK], F32, name=f"pa{jt}", offset=ARR_AT - SLOT if jt == 2 else PA_AT + SLOT * jt)
             arr = stream(jt, rel[jt, 0])
-            if jt == 0:
-                for c in range(2):
-                    nc.vector.tensor_tensor(pa[:, c], arr, ent[jt][:, c], MULT)
+            if jt in HALVED:
+                nc.vector.tensor_tensor(pa[:, 0], arr, ent[jt][:, 0], MULT)
             else:
                 nc.vector.tensor_tensor(pa[:], arr.unsqueeze(1).to_broadcast([P, 2, P, PACK]), ent[jt][:], MULT)
             prods[jt] = [pa]
@@ -182,6 +182,8 @@ def tile_list_ckg_none_kernel(tc, tab_words, tab_scales, tab2_words, tab2_scales
             prods[jt].append(pb)
 
         def products_ari(jt):
+            if jt in HALVED:
+                nc.vector.tensor_tensor(prods[jt][0][:, 1], stream(jt, rel[jt, 0]), ent[jt][:, 1], MULT)
             nc.vector.tensor_tensor(prods[jt][1][:, 1], stream(jt, rel[jt, 1]), ent[jt][:, 0], MULT)
 
         def turn(jt):
@@ -191,22 +193,21 @@ def tile_list_ckg_none_kernel(tc, tab_words, tab_scales, tab2_words, tab2_scales
                 h_bf[g] = big.tile([P, 2, len(GROUPS[g]) * P, PACK], BF16, name=f"h_bf{g}", align_bytes=64,
                                    offset=H_AT + SLOT * (0, 1, 1, 3, 1)[g])
             dst = h_bf[g][:, :, jj * P : (jj + 1) * P, :]
-            if jt == TILES - 1:
+            if jt == TILES - 1 or jt in HALVED:
                 for c in range(2):
-                    nc.vector.tensor_tensor(dst[:, c], prods[jt][0][:, c], prods[jt][1][:, c], ADD)
+                    (nc.gpsimd if jt in HALVED else nc.vector).tensor_tensor(dst[:, c], prods[jt][0][:, c], prods[jt][1][:, c], ADD)
                 return
             if jt not in TURNED:
                 nc.gpsimd.tensor_tensor(dst, prods[jt][0][:], prods[jt][1][:], ADD)
                 return
-            banks = [psum.tile([P, PACK, P], F32, name="h_bank", tag="hy", bufs=2) for c in range(2)]
-            for s in range(2):
-                for c in range(2):
+            for c in range(2):
+                bank = psum.tile([P, PACK, P], F32, name="h_bank", tag="hy", bufs=2)
+                for s in range(2):
                     src = prods[jt][s][:, c].rearrange("j a b -> j (a b)")
                     for t in range(PACK):
-                        nc.tensor.matmul(banks[c][:, t, :], src[:, t * P : (t + 1) * P], ident[:], is_transpose=True,
+                        nc.tensor.matmul(bank[:, t, :], src[:, t * P : (t + 1) * P], ident[:], is_transpose=True,
                                          start=(s == 0 and t == 0), stop=(s == 1 and t == PACK - 1))
-            for c in range(2):
-                nc.scalar.copy(dst[:, c], banks[c][:].rearrange("p t j -> p j t"))
+                nc.scalar.copy(dst[:, c], bank[:].rearrange("p t j -> p j t"))
 
         def quantise(g):
             W = len(GROUPS[g]) * P
@@ -226,7 +227,7 @@ def tile_list_ckg_none_kernel(tc, tab_words, tab_scales, tab2_words, tab2_scales
             codes, plane = h_q[g]
             W = len(GROUPS[g]) * P
             j0 = GROUPS[g][0] * P
-            bank = psum.tile([P, 2, W], F32, name="y_bank", tag="e_bank", bufs=2)
+            bank = psum.tile([P, 2, W], F32, name="y_bank", tag="r_bank" if g < 2 else "e_bank", bufs=4 if g < 2 else 2)
             for c in range(2):
                 for nt in range(2):
                     cols = slice(c * N + nt * P, c * N + (nt + 1) * P)
@@ -243,7 +244,6 @@ def tile_list_ckg_none_kernel(tc, tab_words, tab_scales, tab2_words, tab2_scales
                 relation(jt, c)
         for jt in range(TILES):
             products_arr(jt)
-            products_ari_negated(jt)
             if jt == 5:
                 n_codes = big.tile([P, 2 * N], U32, name="n_codes", align_bytes=64, offset=ARR_AT + SLOT // 4)
                 nc.vector.quantize_mx(out=n_codes[:].bitcast(FP8X4), scales=n_plane[:],
@@ -251,10 +251,11 @@ def tile_list_ckg_none_kernel(tc, tab_words, tab_scales, tab2_words, tab2_scales
                 quantise(0)
                 quantise(1)
                 turn(4)
+            products_ari_negated(jt)
             products_ari(jt)
             if jt == 7:
-                for g in QUANTISE_IN[jt]:
-                    quantise(g)
+                quantise(2)
+                quantise(3)
             if jt + AHEAD < TILES:
                 for stage in ((entity, relation) if jt + AHEAD == SHARED else (relation, entity)):
                     for c in range(2):
@@ -263,10 +264,14 @@ def tile_list_ckg_none_kernel(tc, tab_words, tab_scales, tab2_words, tab2_scales
                 for h in range(2):
                     cols = slice(h * P, (h + 1) * P)
                     nc.scalar.copy(n_bf[:, jt - 1, cols, :], n_raw[jt - 1][:, :, cols].rearrange("p t n -> p n t"))
+            if jt == 6:
+                score(0)
+            if jt == 7:
+                score(2)
+                score(3)
             if jt != 4:
                 turn(jt)
-            for g in QUANTISE_IN.get(jt, ()):
-                score(g)
-        for g in (3, 4):
-            quantise(g)
-            score(g)
+            if jt == 6:
+                score(1)
+        quantise(4)
+        score(4)

@@ -274,4 +274,17 @@ def tile_list_ckg_none_kernel(tc, tab_words, tab_scales, tab2_words, tab2_scales
             if jt == 6:
                 score(1)
         quantise(4)
-        score(4)
+        codes, plane = h_q[4]
+        banks = [psum.tile([P, P], F32, name=f"y_last{nt}", tag="hy", bufs=2) for nt in range(2)]
+        for c in range(2):
+            for nt in range(2):
+                cols = slice(c * N + nt * P, c * N + (nt + 1) * P)
+                nc.tensor.matmul_mx(out=banks[nt][:], lhsT=n_codes[:, cols].bitcast(FP8X4), lhsT_scale=n_plane[:, cols],
+                                    rhs=codes[:, c, :].bitcast(FP8X4), rhs_scale=plane[:, c, :], start=(c == 0), stop=(c == 1))
+        for nt in range(2):
+            y = keep.tile([P, P], F32, name=f"y_last_sb{nt}")
+            if nt == 0:
+                nc.scalar.copy(y[:], banks[nt][:])
+            else:
+                nc.vector.tensor_copy(y[:], banks[nt][:])
+            (nc.scalar, nc.sync)[nt].dma_start(out=out[nt * P : (nt + 1) * P, J - P :], in_=y[:])

@@ -30,7 +30,6 @@ LEAD = T // 8
 S_AT = 46 * T
 G_AT = ((10 * T - 3 * R, 10 * T + 3 * R), (12 * T, 13 * T))
 W_AT = (10 * T + R, S_AT + R)
-NR_AT = (S_AT + R - 16 * N, S_AT + 3 * R)
 TURNED = (3, 6)
 GROUPS = ((0, 1), (2, 3), (4, 5), (6,), (7,))
 SHARED = 3
@@ -91,10 +90,10 @@ def tile_list_ckg_none_kernel(tc, tab_words, tab_scales, tab2_words, tab2_scales
                               s_raw[:].rearrange("p w (m t) -> p w t m", t=PACK))
         nc.vector.tensor_copy(plane_all[:, 4 * R :].bitcast(I32), g_plane[:].bitcast(I32))
         for r in range(1, 4):
-            nc.sync.dma_start(out=plane_all[r:P:32, :].bitcast(I32), in_=plane_all[8 * r : P : 32, :].bitcast(I32))
+            nc.scalar.dma_start(out=plane_all[r:P:32, :].bitcast(I32), in_=plane_all[8 * r : P : 32, :].bitcast(I32))
         for i, w in enumerate((2, 3)):
             w_raw[w] = big.tile([P, R // 2], I32, name=f"w_raw{w}", align_bytes=64, offset=W_AT[i])
-            nc.sync.dma_start(out=w_raw[w][:], in_=w_src[w][0].bitcast(I32))
+            (nc.sync, nc.scalar)[i].dma_start(out=w_raw[w][:], in_=w_src[w][0].bitcast(I32))
 
         def deal(w):
             w_words[w] = keep.tile([P, PACK, P // 2], I32, name=f"w_words{w}", align_bytes=64)
@@ -113,7 +112,7 @@ def tile_list_ckg_none_kernel(tc, tab_words, tab_scales, tab2_words, tab2_scales
         deal(2)
         gather_words(1, 1)
         deal(3)
-        n_raw = [big.tile([P, PACK, N], F32, name=f"n_raw{i}", align_bytes=64, offset=NR_AT[i]) for i in range(2)]
+        n_raw = [big.tile([P, PACK, N], F32, name=f"n_raw{i}", align_bytes=64, offset=16 * N * i) for i in range(2)]
         for c, src in enumerate((nr, ni)):
             for i in range(4):
                 nc.sync.dma_start(out=n_raw[c][i:P:4], in_=src.rearrange("(m t i) n -> i m t n", t=PACK, i=4)[i])

@@ -20,21 +20,14 @@ ADD = mybir.AluOpType.add
 P = 128
 PACK = 4
 HALF = J // 2
-TILES = J // P
-AHEAD = 2
-SLOT = 4096
-PA_AT, PB_AT = 18 * T, 26 * T
-N_AT, ARR_AT, H_AT = 34 * T, 36 * T, 38 * T
-CODES_AT = (ARR_AT - SLOT // 4, N_AT, PB_AT + 5 * SLOT, PA_AT + 5 * SLOT, PB_AT)
+KB = 1024
+BANK = 2 * KB
 LEAD = T // 8
-S_AT = 46 * T
-G_AT = ((10 * T - 3 * R, 10 * T + 3 * R), (12 * T, 13 * T))
-W_AT = (10 * T + R, S_AT + R)
-TURNED = (3, 6)
+TURNED = (0, 3, 6)
+SHARED = (0, 3)
 GROUPS = ((0, 1), (2, 3), (4, 5), (6,), (7,))
-SHARED = 3
-HALVED = (0, 1)
 GROUP_OF = {jt: g for g, tiles in enumerate(GROUPS) for jt in tiles}
+WIN_AT, PICK_AT, S_AT, PROD2_AT, H23_AT, ENT4_AT = 32 * KB, 42 * KB, 46 * KB, 48 * KB, 56 * KB, 60 * KB
 
 
 def tile_list_ckg_none_kernel(tc, tab_words, tab_scales, tab2_words, tab2_scales, wer_words, wer_scales, wei_words,
@@ -43,247 +36,291 @@ def tile_list_ckg_none_kernel(tc, tab_words, tab_scales, tab2_words, tab2_scales
     with ExitStack() as ctx:
         keep = ctx.enter_context(tc.tile_pool(name="keep", bufs=1))
         big = ctx.enter_context(tc.tile_pool(name="big", bufs=1))
-        ring = ctx.enter_context(tc.tile_pool(name="ring", bufs=2))
         psum = ctx.enter_context(tc.psum_pool(name="psum", bufs=1))
 
         lists = [keep.tile([P, J // 16], U16, name=f"list{i}") for i in range(2)]
         words = [big.tile([P, T], I32, name=f"words{i}", align_bytes=64, offset=4 * T * i) for i in range(2)]
-        planes = [big.tile([P, T], U8, name=f"plane{i}", align_bytes=64, offset=16 * T + T * i) for i in range(2)]
-        w_words = {}
+        wins = [big.tile([P, T], U8, name=f"win{i}", align_bytes=64, offset=WIN_AT + T * i) for i in range(2)]
         s_raw = big.tile([P, 4, R // 4], I32, name="s_raw", align_bytes=64, offset=S_AT)
-        plane_all = keep.tile([P, 4 * R + 2 * J], U8, name="plane_all", align_bytes=64)
+        plane = keep.tile([P, 4 * R + 2 * J], U8, name="plane", align_bytes=64)
 
-        nc.gpsimd.memset(planes[0][:].bitcast(I32), 0)
-        nc.vector.memset(planes[1][:].bitcast(I32), 0)
+        nc.gpsimd.memset(wins[0][:].bitcast(I32), 0)
+        nc.vector.memset(wins[1][:].bitcast(I32), 0)
         nc.vector.memset(s_raw[:], 0)
         ident = keep.tile([P, P], F32, name="ident")
         make_identity(nc, ident[:])
 
         w_src = (wer_words, wei_words, wrr_words, wri_words)
+        w_raw, w_words = {}, {}
         nc.sync.dma_start(lists[0][:], offs)
         nc.sync.dma_start(lists[1][:], offs2)
-        w_raw = {}
         for w in range(2):
-            w_raw[w] = big.tile([P, R // 2], I32, name=f"w_raw{w}", align_bytes=64, offset=15 * T + 2 * R * w)
+            w_raw[w] = keep.tile([P, R // 2], I32, name=f"w_raw{w}", align_bytes=64)
             nc.sync.dma_start(out=w_raw[w][:], in_=w_src[w][0].bitcast(I32))
         tab = tab_words[0].rearrange("p t i -> p (t i)").bitcast(I32)
         nc.sync.dma_start(out=words[0][:, :LEAD], in_=tab[:, :LEAD])
         for i, src in enumerate((tab_scales, tab2_scales)):
-            nc.sync.dma_start(out=planes[i][0:P:8, :].bitcast(I32), in_=src[0].bitcast(I32))
+            nc.sync.dma_start(out=wins[i][0:P:8, :].bitcast(I32), in_=src[0].bitcast(I32))
         nc.sync.dma_start(out=words[0][:, LEAD:], in_=tab[:, LEAD:])
         for i, src in enumerate((wer_scales, wei_scales, wrr_scales, wri_scales)):
             nc.sync.dma_start(out=s_raw[0:P:8, i, :], in_=src[0].bitcast(I32))
         nc.sync.dma_start(out=words[1][:], in_=tab2_words[0].rearrange("p t i -> p (t i)").bitcast(I32))
 
         g_words = {}
-        g_plane = big.tile([P, 2 * J], U8, name="g_plane", align_bytes=64, offset=10 * T)
+        picked = big.tile([P, 2 * J], U8, name="picked", align_bytes=64, offset=PICK_AT)
 
         def gather_words(i, h):
             cols = HALF // 16
-            g_words[i, h] = big.tile([P, HALF], U32, name=f"g_words{i}{h}", align_bytes=64,
-                                     offset=G_AT[i][h])
+            if i == 0:
+                g_words[i, h] = big.tile([P, HALF], U32, name=f"g_words{i}{h}", align_bytes=64, offset=PICK_AT + (-3 * R, 3 * R)[h])
+            else:
+                g_words[i, h] = keep.tile([P, HALF], U32, name=f"g_words{i}{h}", align_bytes=64)
             nc.vector.tensor_copy(g_words[i, h][:], words[i][:].bitcast(U32).indirect(lists[i][:, h * cols : (h + 1) * cols]))
 
         for i in range(2):
-            nc.vector.tensor_copy(g_plane[:, i * J : (i + 1) * J], planes[i][:].indirect(lists[i][:]))
-        nc.gpsimd.tensor_copy(plane_all[:, 0 : 4 * R].bitcast(I32).rearrange("p (w t m) -> p w t m", w=4, t=PACK),
+            nc.vector.tensor_copy(picked[:, i * J : (i + 1) * J], wins[i][:].indirect(lists[i][:]))
+        nc.gpsimd.tensor_copy(plane[:, 0 : 4 * R].bitcast(I32).rearrange("p (w t m) -> p w t m", w=4, t=PACK),
                               s_raw[:].rearrange("p w (m t) -> p w t m", t=PACK))
-        nc.vector.tensor_copy(plane_all[:, 4 * R :].bitcast(I32), g_plane[:].bitcast(I32))
+        nc.vector.tensor_copy(plane[:, 4 * R :].bitcast(I32), picked[:].bitcast(I32))
         for r in range(1, 4):
-            nc.scalar.dma_start(out=plane_all[r:P:32, :].bitcast(I32), in_=plane_all[8 * r : P : 32, :].bitcast(I32))
+            nc.scalar.dma_start(out=plane[r:P:32, :].bitcast(I32), in_=plane[8 * r : P : 32, :].bitcast(I32))
         for i, w in enumerate((2, 3)):
-            w_raw[w] = big.tile([P, R // 2], I32, name=f"w_raw{w}", align_bytes=64, offset=W_AT[i])
+            w_raw[w] = big.tile([P, R // 2], I32, name=f"w_raw{w}", align_bytes=64, offset=(PICK_AT + R, S_AT + R)[i])
             (nc.sync, nc.scalar)[i].dma_start(out=w_raw[w][:], in_=w_src[w][0].bitcast(I32))
 
-        def deal(w):
+        def deal_words(w, engine):
             w_words[w] = keep.tile([P, PACK, P // 2], I32, name=f"w_words{w}", align_bytes=64)
-            (nc.vector if w < 2 else nc.gpsimd).tensor_copy(w_words[w][:].rearrange("p t (m k) -> p t m k", k=2),
-                                  w_raw[w][:].rearrange("p (m t k) -> p t m k", t=PACK, k=2))
+            engine.tensor_copy(w_words[w][:].rearrange("p t (m k) -> p t m k", k=2),
+                               w_raw[w][:].rearrange("p (m t k) -> p t m k", t=PACK, k=2))
 
-        deal(0)
-        deal(1)
+        deal_words(0, nc.vector)
+        deal_words(1, nc.vector)
         gather_words(0, 0)
         gather_words(0, 1)
-        warm = psum.tile([P, HALF], F32, name="warm", tag="hy", bufs=2)
+        warm = psum.tile([P, HALF], F32, name="warm", offset=7 * BANK)
         for rep in range(4):
-                nc.tensor.matmul_mx(out=warm[:], lhsT=g_words[0, 0][:, rep * P : (rep + 1) * P].bitcast(FP8X4), lhsT_scale=planes[0][:, 0:P],
-                                    rhs=w_words[0][:].rearrange("p t m -> p (t m)").bitcast(U8).bitcast(FP4X4), rhs_scale=planes[0][:, 0:R], start=True, stop=True)
+            nc.tensor.matmul_mx(out=warm[:], lhsT=g_words[0, 0][:, rep * P : (rep + 1) * P].bitcast(FP8X4), lhsT_scale=wins[0][:, 0:P],
+                                rhs=w_words[0][:].rearrange("p t m -> p (t m)").bitcast(U8).bitcast(FP4X4), rhs_scale=wins[0][:, 0:R], start=True, stop=True)
         gather_words(1, 0)
-        deal(2)
+        deal_words(2, nc.gpsimd)
         gather_words(1, 1)
-        deal(3)
+        deal_words(3, nc.gpsimd)
         n_raw = [big.tile([P, PACK, N], F32, name=f"n_raw{i}", align_bytes=64, offset=16 * N * i) for i in range(2)]
         for c, src in enumerate((nr, ni)):
             for i in range(4):
                 nc.sync.dma_start(out=n_raw[c][i:P:4], in_=src.rearrange("(m t i) n -> i m t n", t=PACK, i=4)[i])
+        n_bf = keep.tile([P, 2, N, PACK], BF16, name="n_bf", align_bytes=64)
 
-        n_bf = big.tile([P, 2, N, PACK], BF16, name="n_bf", align_bytes=64, offset=N_AT)
-        n_plane = keep.tile([P, 2 * N], U8, name="n_plane", align_bytes=64)
-
-        def project(tab, w, jt, bank):
+        def project(w, jt, b):
+            tb = w // 2
+            bank = psum.tile([P, PACK, P], F32, name=f"a{w}_{jt}", offset=b * BANK)
             h, c = divmod(jt * P, HALF)
-            s0 = 4 * R + tab * J + jt * P
+            s0 = 4 * R + tb * J + jt * P
             if jt in TURNED:
                 nc.tensor.matmul_mx(out=bank[:].rearrange("j t p -> j (t p)"),
-                                    lhsT=g_words[tab, h][:, c : c + P].bitcast(FP8X4), lhsT_scale=plane_all[:, s0 : s0 + P],
+                                    lhsT=g_words[tb, h][:, c : c + P].bitcast(FP8X4), lhsT_scale=plane[:, s0 : s0 + P],
                                     rhs=w_words[w][:].rearrange("p t m -> p (t m)").bitcast(U8).bitcast(FP4X4),
-                                    rhs_scale=plane_all[:, w * R : (w + 1) * R], start=True, stop=True)
-                return
+                                    rhs_scale=plane[:, w * R : (w + 1) * R], start=True, stop=True)
+                return bank[:].rearrange("j t p -> j (t p)").rearrange("j (a b) -> j a b", b=PACK)
             for t in range(PACK):
                 nc.tensor.matmul_mx(out=bank[:, t, :], lhsT=w_words[w][:, t, :].bitcast(U8).bitcast(FP4X4),
-                                    lhsT_scale=plane_all[:, w * R + t * P : w * R + (t + 1) * P],
-                                    rhs=g_words[tab, h][:, c : c + P].bitcast(FP8X4), rhs_scale=plane_all[:, s0 : s0 + P],
+                                    lhsT_scale=plane[:, w * R + t * P : w * R + (t + 1) * P],
+                                    rhs=g_words[tb, h][:, c : c + P].bitcast(FP8X4), rhs_scale=plane[:, s0 : s0 + P],
                                     start=True, stop=True)
-
-        def stream(jt, bank):
-            if jt in TURNED:
-                return bank[:].rearrange("j t p -> j (t p)").rearrange("j (a b) -> j a b", b=PACK)
             return bank[:].rearrange("p t j -> p j t")
 
-        ent = {}
-        rel = {}
-        prods = {}
-        h_bf = {}
-        h_q = {}
+        ent, arr_sb, rel, pa, pb, h_bf, h_q = {}, {}, {}, {}, {}, {}, {}
 
-        def entity(jt, c):
-            if c == 0:
-                ent[jt] = ring.tile([P, 2, P, PACK], F32, name="ent", bufs=AHEAD + 2)
-            bank = psum.tile([P, PACK, P], F32, name="e_bank", tag="e_bank", bufs=2)
-            project(0, c, jt, bank)
-            nc.scalar.copy(ent[jt][:, c], stream(jt, bank))
+        def entity(jt, c, b):
+            if (jt, c) == (4, 0):
+                ent[jt] = big.tile([P, 2, P, PACK], F32, name="ent4", offset=ENT4_AT)
+            elif c == 0:
+                ent[jt] = keep.tile([P, 2, P, PACK], F32, name=f"ent{jt}")
+            nc.scalar.copy(ent[jt][:, c], project(c, jt, b))
 
-        def relation(jt, c):
-            rel[jt, c] = psum.tile([P, PACK, P], F32, name="r_bank", tag="r_bank", bufs=4)
-            project(1, 2 + c, jt, rel[jt, c])
-            if (jt, c) == (SHARED, 0):
-                arr = big.tile([P, P, PACK], F32, name="arr", align_bytes=64, offset=ARR_AT)
-                nc.scalar.copy(arr[:], stream(jt, rel[jt, c]))
-                pa = big.tile([P, 2, P, PACK], F32, name=f"pa{jt}", offset=PA_AT + SLOT * jt)
-                nc.gpsimd.tensor_tensor(pa[:], arr[:].unsqueeze(1).to_broadcast([P, 2, P, PACK]), ent[jt][:], MULT)
-                prods[jt] = [pa]
+        def arr_out(jt, b):
+            arr_sb[jt] = keep.tile([P, P, PACK], F32, name=f"arr{jt}")
+            nc.scalar.copy(arr_sb[jt][:], project(2, jt, b))
 
-        def products_arr(jt):
-            if jt == SHARED:
-                return
-            pa = big.tile([P, 2, P, PACK], F32, name=f"pa{jt}", offset=ARR_AT - SLOT if jt == 2 else PA_AT + SLOT * jt)
-            arr = stream(jt, rel[jt, 0])
-            if jt in HALVED:
-                nc.vector.tensor_tensor(pa[:, 0], arr, ent[jt][:, 0], MULT)
+        def relation(jt, c, b):
+            rel[jt, c] = project(2 + c, jt, b)
+
+        def prod_tile(name, jt, s):
+            if jt == 2:
+                return big.tile([P, 2, P, PACK], F32, name=name, offset=PROD2_AT + 4 * KB * s)
+            return keep.tile([P, 2, P, PACK], F32, name=name)
+
+        def times_arr(jt):
+            pa[jt] = prod_tile(f"pa{jt}", jt, 0)
+            if jt in SHARED:
+                nc.gpsimd.tensor_tensor(pa[jt][:], arr_sb[jt][:].unsqueeze(1).to_broadcast([P, 2, P, PACK]), ent[jt][:], MULT)
             else:
-                nc.vector.tensor_tensor(pa[:], arr.unsqueeze(1).to_broadcast([P, 2, P, PACK]), ent[jt][:], MULT)
-            prods[jt] = [pa]
+                nc.vector.tensor_tensor(pa[jt][:], rel[jt, 0].unsqueeze(1).to_broadcast([P, 2, P, PACK]), ent[jt][:], MULT)
 
-        def products_ari_negated(jt):
-            pb = big.tile([P, 2, P, PACK], F32, name=f"pb{jt}", offset=ARR_AT + SLOT // 2 if jt == 2 else PB_AT + SLOT * jt)
-            ari = stream(jt, rel[jt, 1])
-            nc.vector.scalar_tensor_tensor(pb[:, 0], ari, -1.0, ent[jt][:, 1], MULT, MULT)
-            prods[jt].append(pb)
+        def times_ari(jt):
+            pb[jt] = prod_tile(f"pb{jt}", jt, 1)
+            nc.vector.scalar_tensor_tensor(pb[jt][:, 0], rel[jt, 1], -1.0, ent[jt][:, 1], MULT, MULT)
+            nc.vector.tensor_tensor(pb[jt][:, 1], rel[jt, 1], ent[jt][:, 0], MULT)
 
-        def products_ari(jt):
-            if jt in HALVED:
-                nc.vector.tensor_tensor(prods[jt][0][:, 1], stream(jt, rel[jt, 0]), ent[jt][:, 1], MULT)
-            nc.vector.tensor_tensor(prods[jt][1][:, 1], stream(jt, rel[jt, 1]), ent[jt][:, 0], MULT)
-
-        def turn(jt):
+        def h_slot(jt):
             g = GROUP_OF[jt]
+            if g not in h_bf:
+                shape = [P, 2, len(GROUPS[g]) * P, PACK]
+                if g in (1, 2):
+                    h_bf[g] = big.tile(shape, BF16, name=f"h_bf{g}", align_bytes=64, offset=H23_AT)
+                else:
+                    h_bf[g] = keep.tile(shape, BF16, name=f"h_bf{g}", align_bytes=64)
             jj = jt - GROUPS[g][0]
-            if jj == 0:
-                h_bf[g] = big.tile([P, 2, len(GROUPS[g]) * P, PACK], BF16, name=f"h_bf{g}", align_bytes=64,
-                                   offset=H_AT + SLOT * (0, 1, 1, 3, 1)[g])
-            dst = h_bf[g][:, :, jj * P : (jj + 1) * P, :]
-            if jt == TILES - 1 or jt in HALVED:
-                for c in range(2):
-                    (nc.gpsimd if jt in HALVED else nc.vector).tensor_tensor(dst[:, c], prods[jt][0][:, c], prods[jt][1][:, c], ADD)
-                return
-            if jt not in TURNED:
-                nc.gpsimd.tensor_tensor(dst, prods[jt][0][:], prods[jt][1][:], ADD)
-                return
-            for c in range(2):
-                bank = psum.tile([P, PACK, P], F32, name="h_bank", tag="hy", bufs=2)
-                for s in range(2):
-                    src = prods[jt][s][:, c].rearrange("j a b -> j (a b)")
-                    for t in range(PACK):
-                        nc.tensor.matmul(bank[:, t, :], src[:, t * P : (t + 1) * P], ident[:], is_transpose=True,
-                                         start=(s == 0 and t == 0), stop=(s == 1 and t == PACK - 1))
-                nc.scalar.copy(dst[:, c], bank[:].rearrange("p t j -> p j t"))
+            return h_bf[g][:, :, jj * P : (jj + 1) * P, :]
 
-        def quantise(g):
+        def add_on_gpsimd(jt):
+            nc.gpsimd.tensor_tensor(h_slot(jt), pa[jt][:], pb[jt][:], ADD)
+
+        def turn(jt, c, b):
+            bank = psum.tile([P, PACK, P], F32, name=f"h{c}_{jt}", offset=b * BANK)
+            for s, prod in enumerate((pb[jt], pa[jt])):
+                src = prod[:, c].rearrange("j a b -> j (a b)")
+                for t in range(PACK):
+                    nc.tensor.matmul(bank[:, t, :], src[:, t * P : (t + 1) * P], ident[:], is_transpose=True,
+                                     start=(s == 0 and t == 0), stop=(s == 1 and t == PACK - 1))
+            nc.scalar.copy(h_slot(jt)[:, c], bank[:].rearrange("p t j -> p j t"))
+
+        def cast_n(c):
+            for h in range(2):
+                cols = slice(h * P, (h + 1) * P)
+                nc.scalar.copy(n_bf[:, c, cols, :], n_raw[c][:, :, cols].rearrange("p t n -> p n t"))
+
+        def quantise(g, c=None):
             W = len(GROUPS[g]) * P
-            codes = big.tile([P, 2, W], U32, name=f"h_codes{g}", align_bytes=64, offset=CODES_AT[g])
-            plane = keep.tile([P, 2, W], U8, name=f"h_plane{g}", align_bytes=64)
-            if g < len(GROUPS) - 1:
+            if g not in h_q:
+                if g == 0:
+                    codes = big.tile([P, 2, W], U32, name="h_codes0", align_bytes=64, offset=PROD2_AT + 4 * KB)
+                else:
+                    codes = keep.tile([P, 2, W], U32, name=f"h_codes{g}", align_bytes=64)
+                if g < 2:
+                    scales = big.tile([P, 2, W], U8, name=f"h_plane{g}", align_bytes=64, offset=ENT4_AT + (g + 1) * KB)
+                else:
+                    scales = keep.tile([P, 2, W], U8, name=f"h_plane{g}", align_bytes=64)
+                h_q[g] = (codes, scales)
+            codes, scales = h_q[g]
+            if c is None:
                 nc.vector.quantize_mx(out=codes[:].rearrange("p c j -> p (c j)").bitcast(FP8X4),
-                                      scales=plane[:].rearrange("p c j -> p (c j)"),
+                                      scales=scales[:].rearrange("p c j -> p (c j)"),
                                       in_=h_bf[g][:].rearrange("p c j t -> p (c j t)"))
             else:
-                for c in range(2):
-                    nc.vector.quantize_mx(out=codes[:, c, :].bitcast(FP8X4), scales=plane[:, c, :],
-                                          in_=h_bf[g][:, c].rearrange("p j t -> p (j t)"))
-            h_q[g] = (codes, plane)
+                nc.vector.quantize_mx(out=codes[:, c, :].bitcast(FP8X4), scales=scales[:, c, :],
+                                      in_=h_bf[g][:, c].rearrange("p j t -> p (j t)"))
 
-        def score(g):
-            codes, plane = h_q[g]
+        def add_on_vector(jt, c):
+            nc.vector.tensor_tensor(h_slot(jt)[:, c], pa[jt][:, c], pb[jt][:, c], ADD)
+
+        n_q = []
+
+        def quantise_n():
+            codes = big.tile([P, 2 * N], U32, name="n_codes", align_bytes=64, offset=PROD2_AT)
+            scales = big.tile([P, 2 * N], U8, name="n_plane", align_bytes=64, offset=ENT4_AT)
+            nc.vector.quantize_mx(out=codes[:].bitcast(FP8X4), scales=scales[:], in_=n_bf[:].rearrange("p c n t -> p (c n t)"))
+            n_q.extend((codes, scales))
+
+        def score_pass(bank, g, c, nt, start, stop):
+            codes, scales = h_q[g]
+            cols = slice(c * N + nt * P, c * N + (nt + 1) * P)
+            nc.tensor.matmul_mx(out=bank, lhsT=n_q[0][:, cols].bitcast(FP8X4), lhsT_scale=n_q[1][:, cols],
+                                rhs=codes[:, c, :].bitcast(FP8X4), rhs_scale=scales[:, c, :], start=start, stop=stop)
+
+        def score(g, b):
             W = len(GROUPS[g]) * P
             j0 = GROUPS[g][0] * P
-            bank = psum.tile([P, 2, W], F32, name="y_bank", tag="r_bank" if g < 2 else "e_bank", bufs=4 if g < 2 else 2)
+            bank = psum.tile([P, 2, W], F32, name=f"y_bank{g}", offset=b * BANK)
             for c in range(2):
                 for nt in range(2):
-                    cols = slice(c * N + nt * P, c * N + (nt + 1) * P)
-                    nc.tensor.matmul_mx(out=bank[:, nt, :], lhsT=n_codes[:, cols].bitcast(FP8X4), lhsT_scale=n_plane[:, cols],
-                                        rhs=codes[:, c, :].bitcast(FP8X4), rhs_scale=plane[:, c, :],
-                                        start=(c == 0 and nt == 0), stop=(c == 1 and nt == 1))
-            y = ring.tile([P, 2, W], F32, name="y", bufs=len(GROUPS))
+                    score_pass(bank[:, nt, :], g, c, nt, c == 0 and nt == 0, c == 1 and nt == 1)
+            y = keep.tile([P, 2, W], F32, name=f"y{g}")
             nc.scalar.copy(y[:], bank[:])
             nc.sync.dma_start(out=out.rearrange("(nt p) j -> p nt j", p=P)[:, :, j0 : j0 + W], in_=y[:])
 
-        for jt in range(AHEAD):
+        def score_last(b0, b1):
+            banks = [psum.tile([P, P], F32, name=f"y_last{nt}", offset=(b0, b1)[nt] * BANK) for nt in range(2)]
             for c in range(2):
-                entity(jt, c)
-                relation(jt, c)
-        for jt in range(TILES):
-            products_arr(jt)
-            if jt == 5:
-                n_codes = big.tile([P, 2 * N], U32, name="n_codes", align_bytes=64, offset=ARR_AT + SLOT // 4)
-                nc.vector.quantize_mx(out=n_codes[:].bitcast(FP8X4), scales=n_plane[:],
-                                      in_=n_bf[:].rearrange("p c n t -> p (c n t)"))
-                quantise(0)
-                quantise(1)
-                turn(4)
-            products_ari_negated(jt)
-            products_ari(jt)
-            if jt == 7:
-                quantise(2)
-                quantise(3)
-            if jt + AHEAD < TILES:
-                for stage in ((entity, relation) if jt + AHEAD == SHARED else (relation, entity)):
-                    for c in range(2):
-                        stage(jt + AHEAD, c)
-            if jt in (1, 2):
-                for h in range(2):
-                    cols = slice(h * P, (h + 1) * P)
-                    nc.scalar.copy(n_bf[:, jt - 1, cols, :], n_raw[jt - 1][:, :, cols].rearrange("p t n -> p n t"))
-            if jt == 6:
-                score(0)
-            if jt == 7:
-                score(2)
-                score(3)
-            if jt != 4:
-                turn(jt)
-            if jt == 6:
-                score(1)
-        quantise(4)
-        codes, plane = h_q[4]
-        banks = [psum.tile([P, P], F32, name=f"y_last{nt}", tag="hy", bufs=2) for nt in range(2)]
-        for c in range(2):
+                for nt in range(2):
+                    score_pass(banks[nt][:], len(GROUPS) - 1, c, nt, c == 0, c == 1)
             for nt in range(2):
-                cols = slice(c * N + nt * P, c * N + (nt + 1) * P)
-                nc.tensor.matmul_mx(out=banks[nt][:], lhsT=n_codes[:, cols].bitcast(FP8X4), lhsT_scale=n_plane[:, cols],
-                                    rhs=codes[:, c, :].bitcast(FP8X4), rhs_scale=plane[:, c, :], start=(c == 0), stop=(c == 1))
-        for nt in range(2):
-            y = keep.tile([P, P], F32, name=f"y_last_sb{nt}")
-            if nt == 0:
-                nc.scalar.copy(y[:], banks[nt][:])
-            else:
-                nc.vector.tensor_copy(y[:], banks[nt][:])
-            (nc.scalar, nc.sync)[nt].dma_start(out=out[nt * P : (nt + 1) * P, J - P :], in_=y[:])
+                y = keep.tile([P, P], F32, name=f"y_last_sb{nt}")
+                if nt == 0:
+                    nc.scalar.copy(y[:], banks[nt][:])
+                else:
+                    nc.vector.tensor_copy(y[:], banks[nt][:])
+                (nc.scalar, nc.sync)[nt].dma_start(out=out[nt * P : (nt + 1) * P, J - P :], in_=y[:])
+
+        for k in range(4):
+            entity(k // 2, k % 2, k)
+        arr_out(0, 0)
+        relation(0, 1, 1)
+        entity(3, 0, 4)
+        entity(3, 1, 5)
+        relation(1, 0, 2)
+        arr_out(3, 6)
+        relation(1, 1, 3)
+        times_arr(0)
+        times_ari(0)
+        entity(2, 0, 0)
+        entity(2, 1, 6)
+        relation(2, 0, 7)
+        relation(2, 1, 1)
+        times_arr(1)
+        times_ari(1)
+        times_arr(3)
+        relation(3, 1, 4)
+        turn(0, 0, 2)
+        entity(4, 0, 0)
+        entity(4, 1, 6)
+        turn(0, 1, 3)
+        add_on_gpsimd(1)
+        times_arr(2)
+        relation(4, 0, 2)
+        times_ari(2)
+        relation(4, 1, 1)
+        relation(5, 0, 3)
+        relation(5, 1, 7)
+        entity(5, 0, 0)
+        entity(5, 1, 6)
+        add_on_gpsimd(2)
+        times_ari(3)
+        turn(3, 0, 4)
+        turn(3, 1, 5)
+        cast_n(0)
+        cast_n(1)
+        times_arr(4)
+        times_ari(4)
+        relation(6, 1, 4)
+        entity(6, 0, 2)
+        entity(6, 1, 1)
+        times_arr(5)
+        relation(6, 0, 3)
+        quantise_n()
+        quantise(0)
+        quantise(1)
+        add_on_gpsimd(4)
+        times_ari(5)
+        add_on_gpsimd(5)
+        score(0, 0)
+        entity(7, 0, 2)
+        entity(7, 1, 5)
+        relation(7, 0, 7)
+        times_arr(6)
+        relation(7, 1, 3)
+        times_ari(6)
+        turn(6, 0, 4)
+        turn(6, 1, 5)
+        times_arr(7)
+        score(1, 7)
+        times_ari(7)
+        add_on_vector(7, 0)
+        quantise(2)
+        score(2, 0)
+        quantise(3)
+        score(3, 6)
+        add_on_vector(7, 1)
+        quantise(4, 0)
+        quantise(4, 1)
+        score_last(2, 1)

@@ -23,11 +23,11 @@ HALF = J // 2
 KB = 1024
 BANK = 2 * KB
 LEAD = T // 8
-TURNED = (0, 3, 6)
-SHARED = (0, 3)
+TURNED = (3, 4, 5, 6)
+SHARED = (3, 5)
 GROUPS = ((0, 1), (2, 3), (4, 5), (6,), (7,))
 GROUP_OF = {jt: g for g, tiles in enumerate(GROUPS) for jt in tiles}
-WIN_AT, PICK_AT, S_AT, PROD2_AT, H23_AT, ENT4_AT = 32 * KB, 42 * KB, 46 * KB, 48 * KB, 56 * KB, 60 * KB
+WIN_AT, PICK_AT, S_AT, PROD2_AT, H23_AT, ENT6_AT = 32 * KB, 42 * KB, 46 * KB, 48 * KB, 56 * KB, 60 * KB
 
 
 def tile_list_ckg_none_kernel(tc, tab_words, tab_scales, tab2_words, tab2_scales, wer_words, wer_scales, wei_words,
@@ -132,8 +132,8 @@ def tile_list_ckg_none_kernel(tc, tab_words, tab_scales, tab2_words, tab2_scales
         ent, arr_sb, rel, pa, pb, h_bf, h_q = {}, {}, {}, {}, {}, {}, {}
 
         def entity(jt, c, b):
-            if (jt, c) == (4, 0):
-                ent[jt] = big.tile([P, 2, P, PACK], F32, name="ent4", offset=ENT4_AT)
+            if (jt, c) == (6, 0):
+                ent[jt] = big.tile([P, 2, P, PACK], F32, name="ent6", offset=ENT6_AT)
             elif c == 0:
                 ent[jt] = keep.tile([P, 2, P, PACK], F32, name=f"ent{jt}")
             nc.scalar.copy(ent[jt][:, c], project(c, jt, b))
@@ -150,31 +150,40 @@ def tile_list_ckg_none_kernel(tc, tab_words, tab_scales, tab2_words, tab2_scales
                 return big.tile([P, 2, P, PACK], F32, name=name, offset=PROD2_AT + 4 * KB * s)
             return keep.tile([P, 2, P, PACK], F32, name=name)
 
-        def times_arr(jt):
-            pa[jt] = prod_tile(f"pa{jt}", jt, 0)
+        def times_arr(jt, c=None):
+            if jt not in pa:
+                pa[jt] = prod_tile(f"pa{jt}", jt, 0)
             if jt in SHARED:
                 nc.gpsimd.tensor_tensor(pa[jt][:], arr_sb[jt][:].unsqueeze(1).to_broadcast([P, 2, P, PACK]), ent[jt][:], MULT)
-            else:
+            elif c is None:
                 nc.vector.tensor_tensor(pa[jt][:], rel[jt, 0].unsqueeze(1).to_broadcast([P, 2, P, PACK]), ent[jt][:], MULT)
+            else:
+                nc.vector.tensor_tensor(pa[jt][:, c], rel[jt, 0], ent[jt][:, c], MULT)
 
-        def times_ari(jt):
-            pb[jt] = prod_tile(f"pb{jt}", jt, 1)
-            nc.vector.scalar_tensor_tensor(pb[jt][:, 0], rel[jt, 1], -1.0, ent[jt][:, 1], MULT, MULT)
-            nc.vector.tensor_tensor(pb[jt][:, 1], rel[jt, 1], ent[jt][:, 0], MULT)
+        def times_ari(jt, c=None):
+            if jt not in pb:
+                pb[jt] = prod_tile(f"pb{jt}", jt, 1)
+            if c != 1:
+                nc.vector.scalar_tensor_tensor(pb[jt][:, 0], rel[jt, 1], -1.0, ent[jt][:, 1], MULT, MULT)
+            if c != 0:
+                nc.vector.tensor_tensor(pb[jt][:, 1], rel[jt, 1], ent[jt][:, 0], MULT)
 
         def h_slot(jt):
             g = GROUP_OF[jt]
             if g not in h_bf:
                 shape = [P, 2, len(GROUPS[g]) * P, PACK]
-                if g in (1, 2):
+                if g == 1:
                     h_bf[g] = big.tile(shape, BF16, name=f"h_bf{g}", align_bytes=64, offset=H23_AT)
                 else:
                     h_bf[g] = keep.tile(shape, BF16, name=f"h_bf{g}", align_bytes=64)
             jj = jt - GROUPS[g][0]
             return h_bf[g][:, :, jj * P : (jj + 1) * P, :]
 
-        def add_on_gpsimd(jt):
-            nc.gpsimd.tensor_tensor(h_slot(jt), pa[jt][:], pb[jt][:], ADD)
+        def add_on_gpsimd(jt, c=None):
+            if c is None:
+                nc.gpsimd.tensor_tensor(h_slot(jt), pa[jt][:], pb[jt][:], ADD)
+            else:
+                nc.gpsimd.tensor_tensor(h_slot(jt)[:, c], pa[jt][:, c], pb[jt][:, c], ADD)
 
         def turn(jt, c, b):
             bank = psum.tile([P, PACK, P], F32, name=f"h{c}_{jt}", offset=b * BANK)
@@ -198,7 +207,7 @@ def tile_list_ckg_none_kernel(tc, tab_words, tab_scales, tab2_words, tab2_scales
                 else:
                     codes = keep.tile([P, 2, W], U32, name=f"h_codes{g}", align_bytes=64)
                 if g < 2:
-                    scales = big.tile([P, 2, W], U8, name=f"h_plane{g}", align_bytes=64, offset=ENT4_AT + (g + 1) * KB)
+                    scales = big.tile([P, 2, W], U8, name=f"h_plane{g}", align_bytes=64, offset=ENT6_AT + (g + 1) * KB)
                 else:
                     scales = keep.tile([P, 2, W], U8, name=f"h_plane{g}", align_bytes=64)
                 h_q[g] = (codes, scales)
@@ -218,7 +227,7 @@ def tile_list_ckg_none_kernel(tc, tab_words, tab_scales, tab2_words, tab2_scales
 
         def quantise_n():
             codes = big.tile([P, 2 * N], U32, name="n_codes", align_bytes=64, offset=PROD2_AT)
-            scales = big.tile([P, 2 * N], U8, name="n_plane", align_bytes=64, offset=ENT4_AT)
+            scales = big.tile([P, 2 * N], U8, name="n_plane", align_bytes=64, offset=ENT6_AT)
             nc.vector.quantize_mx(out=codes[:].bitcast(FP8X4), scales=scales[:], in_=n_bf[:].rearrange("p c n t -> p (c n t)"))
             n_q.extend((codes, scales))
 
@@ -252,75 +261,79 @@ def tile_list_ckg_none_kernel(tc, tab_words, tab_scales, tab2_words, tab2_scales
                     nc.vector.tensor_copy(y[:], banks[nt][:])
                 (nc.scalar, nc.sync)[nt].dma_start(out=out[nt * P : (nt + 1) * P, J - P :], in_=y[:])
 
-        for k in range(4):
-            entity(k // 2, k % 2, k)
-        arr_out(0, 0)
+        entity(0, 0, 4)
+        relation(0, 0, 0)
+        entity(0, 1, 5)
         relation(0, 1, 1)
-        entity(3, 0, 4)
-        entity(3, 1, 5)
+        entity(1, 0, 6)
         relation(1, 0, 2)
-        arr_out(3, 6)
+        entity(1, 1, 7)
         relation(1, 1, 3)
-        times_arr(0)
-        times_ari(0)
-        entity(2, 0, 0)
-        entity(2, 1, 6)
-        relation(2, 0, 7)
-        relation(2, 1, 1)
-        times_arr(1)
-        times_ari(1)
+        for jt in range(2):
+            times_arr(jt, 0)
+            times_ari(jt, 0)
+            add_on_gpsimd(jt, 0)
+            times_arr(jt, 1)
+            relation(2 + jt, jt, 2 * jt)
+            times_ari(jt, 1)
+            add_on_gpsimd(jt, 1)
+            if jt == 0:
+                relation(2, 1, 1)
+                entity(2, 0, 4)
+                entity(2, 1, 5)
+                entity(3, 0, 6)
+                entity(3, 1, 7)
+        arr_out(3, 3)
         times_arr(3)
-        relation(3, 1, 4)
-        turn(0, 0, 2)
-        entity(4, 0, 0)
-        entity(4, 1, 6)
-        turn(0, 1, 3)
-        add_on_gpsimd(1)
         times_arr(2)
-        relation(4, 0, 2)
+        relation(4, 0, 0)
+        entity(4, 0, 4)
+        entity(4, 1, 5)
         times_ari(2)
         relation(4, 1, 1)
-        relation(5, 0, 3)
-        relation(5, 1, 7)
-        entity(5, 0, 0)
-        entity(5, 1, 6)
+        entity(5, 0, 4)
+        entity(5, 1, 5)
+        arr_out(5, 3)
+        times_arr(5)
         add_on_gpsimd(2)
         times_ari(3)
-        turn(3, 0, 4)
-        turn(3, 1, 5)
+        relation(5, 1, 2)
+        times_arr(4)
+        relation(6, 0, 0)
+        entity(6, 0, 4)
+        entity(6, 1, 5)
+        times_ari(4)
+        relation(6, 1, 1)
+        turn(3, 0, 6)
+        turn(3, 1, 7)
         cast_n(0)
         cast_n(1)
-        times_arr(4)
-        times_ari(4)
-        relation(6, 1, 4)
-        entity(6, 0, 2)
-        entity(6, 1, 1)
-        times_arr(5)
-        relation(6, 0, 3)
+        times_ari(5)
+        entity(7, 0, 6)
+        entity(7, 1, 7)
+        turn(4, 0, 2)
+        turn(4, 1, 3)
+        times_arr(6)
+        relation(7, 1, 0)
+        turn(5, 0, 4)
+        turn(5, 1, 5)
+        times_ari(6)
+        relation(7, 0, 1)
         quantise_n()
         quantise(0)
         quantise(1)
-        add_on_gpsimd(4)
-        times_ari(5)
-        add_on_gpsimd(5)
-        score(0, 0)
-        entity(7, 0, 2)
-        entity(7, 1, 5)
-        relation(7, 0, 7)
-        times_arr(6)
-        relation(7, 1, 3)
-        times_ari(6)
-        turn(6, 0, 4)
-        turn(6, 1, 5)
+        score(0, 6)
+        score(1, 2)
+        turn(6, 0, 7)
+        turn(6, 1, 3)
         times_arr(7)
-        score(1, 7)
-        times_ari(7)
-        add_on_vector(7, 0)
         quantise(2)
-        score(2, 0)
+        times_ari(7)
+        score(2, 1)
+        add_on_vector(7, 0)
         quantise(3)
         score(3, 6)
         add_on_vector(7, 1)
         quantise(4, 0)
         quantise(4, 1)
-        score_last(2, 1)
+        score_last(0, 4)

@@ -23,11 +23,11 @@ HALF = J // 2
 KB = 1024
 BANK = 2 * KB
 LEAD = T // 8
-TURNED = (3, 4, 5, 6)
+TURNED = (2, 3, 5, 6)
 SHARED = (3, 5)
 GROUPS = ((0, 1), (2, 3), (4, 5), (6,), (7,))
 GROUP_OF = {jt: g for g, tiles in enumerate(GROUPS) for jt in tiles}
-WIN_AT, PICK_AT, S_AT, PROD2_AT, H23_AT, ENT6_AT = 32 * KB, 42 * KB, 46 * KB, 48 * KB, 56 * KB, 60 * KB
+WIN_AT, PICK_AT, S_AT, PROD4_AT, H23_AT, ENT6_AT = 32 * KB, 42 * KB, 46 * KB, 48 * KB, 56 * KB, 60 * KB
 
 
 def tile_list_ckg_none_kernel(tc, tab_words, tab_scales, tab2_words, tab2_scales, wer_words, wer_scales, wei_words,
@@ -146,8 +146,8 @@ def tile_list_ckg_none_kernel(tc, tab_words, tab_scales, tab2_words, tab2_scales
             rel[jt, c] = project(2 + c, jt, b)
 
         def prod_tile(name, jt, s):
-            if jt == 2:
-                return big.tile([P, 2, P, PACK], F32, name=name, offset=PROD2_AT + 4 * KB * s)
+            if jt == 4:
+                return big.tile([P, 2, P, PACK], F32, name=name, offset=PROD4_AT + 4 * KB * s)
             return keep.tile([P, 2, P, PACK], F32, name=name)
 
         def times_arr(jt, c=None):
@@ -203,7 +203,7 @@ def tile_list_ckg_none_kernel(tc, tab_words, tab_scales, tab2_words, tab2_scales
             W = len(GROUPS[g]) * P
             if g not in h_q:
                 if g == 0:
-                    codes = big.tile([P, 2, W], U32, name="h_codes0", align_bytes=64, offset=PROD2_AT + 4 * KB)
+                    codes = big.tile([P, 2, W], U32, name="h_codes0", align_bytes=64, offset=PROD4_AT + 4 * KB)
                 else:
                     codes = keep.tile([P, 2, W], U32, name=f"h_codes{g}", align_bytes=64)
                 if g < 2:
@@ -226,7 +226,7 @@ def tile_list_ckg_none_kernel(tc, tab_words, tab_scales, tab2_words, tab2_scales
         n_q = []
 
         def quantise_n():
-            codes = big.tile([P, 2 * N], U32, name="n_codes", align_bytes=64, offset=PROD2_AT)
+            codes = big.tile([P, 2 * N], U32, name="n_codes", align_bytes=64, offset=PROD4_AT)
             scales = big.tile([P, 2 * N], U8, name="n_plane", align_bytes=64, offset=ENT6_AT)
             nc.vector.quantize_mx(out=codes[:].bitcast(FP8X4), scales=scales[:], in_=n_bf[:].rearrange("p c n t -> p (c n t)"))
             n_q.extend((codes, scales))
@@ -295,45 +295,46 @@ def tile_list_ckg_none_kernel(tc, tab_words, tab_scales, tab2_words, tab2_scales
         entity(5, 1, 5)
         arr_out(5, 3)
         times_arr(5)
-        add_on_gpsimd(2)
         times_ari(3)
         relation(5, 1, 2)
         times_arr(4)
         relation(6, 0, 0)
         entity(6, 0, 4)
         entity(6, 1, 5)
+        turn(2, 0, 6)
+        turn(2, 1, 7)
         times_ari(4)
+        add_on_gpsimd(4)
         relation(6, 1, 1)
-        turn(3, 0, 6)
-        turn(3, 1, 7)
+        relation(7, 1, 3)
+        entity(7, 0, 4)
+        entity(7, 1, 5)
         cast_n(0)
         cast_n(1)
+        turn(3, 0, 6)
+        turn(3, 1, 7)
         times_ari(5)
-        entity(7, 0, 6)
-        entity(7, 1, 7)
-        turn(4, 0, 2)
-        turn(4, 1, 3)
-        times_arr(6)
-        relation(7, 1, 0)
+        relation(7, 0, 2)
         turn(5, 0, 4)
         turn(5, 1, 5)
+        times_arr(6)
         times_ari(6)
-        relation(7, 0, 1)
+        turn(6, 0, 6)
+        turn(6, 1, 7)
+        times_arr(7)
         quantise_n()
         quantise(0)
+        score(0, 0)
+        times_ari(7, 0)
         quantise(1)
-        score(0, 6)
-        score(1, 2)
-        turn(6, 0, 7)
-        turn(6, 1, 3)
-        times_arr(7)
+        score(1, 1)
+        times_ari(7, 1)
         quantise(2)
-        times_ari(7)
-        score(2, 1)
-        add_on_vector(7, 0)
+        score(2, 2)
         quantise(3)
-        score(3, 6)
+        score(3, 4)
+        add_on_vector(7, 0)
         add_on_vector(7, 1)
         quantise(4, 0)
         quantise(4, 1)
-        score_last(0, 4)
+        score_last(0, 5)

@@ -22,12 +22,15 @@ PACK = 4
 HALF = J // 2
 KB = 1024
 BANK = 2 * KB
-LEAD = T // 8
-TURNED = (2, 3, 5, 6)
-SHARED = (3, 5)
+CUTS = (0, T // 8, 3 * T // 8, T)
+PICKS = (((0, 0),), ((1, 0),), ((0, 1), (1, 1)))
+PICK_PLACE = {key: (g, k) for g, keys in enumerate(PICKS) for k, key in enumerate(keys)}
+TURNED = (1, 3, 4, 5, 6)
+SHARED = (1, 3, 4)
 GROUPS = ((0, 1), (2, 3), (4, 5), (6,), (7,))
 GROUP_OF = {jt: g for g, tiles in enumerate(GROUPS) for jt in tiles}
-WIN_AT, PICK_AT, S_AT, PROD4_AT, H23_AT, ENT6_AT = 32 * KB, 42 * KB, 46 * KB, 48 * KB, 56 * KB, 60 * KB
+TAB_AT, W3_AT = (0, 20 * KB), 19 * KB - 256
+WIN_AT, PICK_AT, S_AT, PROD4_AT, H23_AT, ENT6_AT = 38 * KB, (36 * KB - 256, 36 * KB, 36 * KB + 512), (20 * KB - 512, 46 * KB), 48 * KB, 56 * KB, 60 * KB
 
 
 def tile_list_ckg_none_kernel(tc, tab_words, tab_scales, tab2_words, tab2_scales, wer_words, wer_scales, wei_words,
@@ -39,72 +42,90 @@ def tile_list_ckg_none_kernel(tc, tab_words, tab_scales, tab2_words, tab2_scales
         psum = ctx.enter_context(tc.psum_pool(name="psum", bufs=1))
 
         lists = [keep.tile([P, J // 16], U16, name=f"list{i}") for i in range(2)]
-        words = [big.tile([P, T], I32, name=f"words{i}", align_bytes=64, offset=4 * T * i) for i in range(2)]
+        words = [big.tile([P, T], I32, name=f"words{i}", align_bytes=64, offset=TAB_AT[i]) for i in range(2)]
         wins = [big.tile([P, T], U8, name=f"win{i}", align_bytes=64, offset=WIN_AT + T * i) for i in range(2)]
-        s_raw = big.tile([P, 4, R // 4], I32, name="s_raw", align_bytes=64, offset=S_AT)
-        plane = keep.tile([P, 4 * R + 2 * J], U8, name="plane", align_bytes=64)
+        s_raw = [big.tile([P, 2, R // 4], I32, name=f"s_raw{g}", align_bytes=64, offset=S_AT[g]) for g in range(2)]
+        planes = [keep.tile([P, (HALF + 2 * R, HALF + 2 * R, J)[g]], U8, name=f"plane{g}", align_bytes=64) for g in range(3)]
 
         nc.gpsimd.memset(wins[0][:].bitcast(I32), 0)
+        for g in range(2):
+            nc.vector.memset(s_raw[g][:], 0)
         nc.vector.memset(wins[1][:].bitcast(I32), 0)
-        nc.vector.memset(s_raw[:], 0)
         ident = keep.tile([P, P], F32, name="ident")
         make_identity(nc, ident[:])
 
         w_src = (wer_words, wei_words, wrr_words, wri_words)
+        s_src = (wer_scales, wei_scales, wrr_scales, wri_scales)
         w_raw, w_words = {}, {}
+        tab = tab_words[0].rearrange("p t i -> p (t i)").bitcast(I32)
+
+        def load_weight(w, at=None):
+            if at is None:
+                w_raw[w] = keep.tile([P, R // 2], I32, name=f"w_raw{w}", align_bytes=64)
+            else:
+                w_raw[w] = big.tile([P, R // 2], I32, name=f"w_raw{w}", align_bytes=64, offset=at)
+            nc.sync.dma_start(out=w_raw[w][:], in_=w_src[w][0].bitcast(I32))
+
+        def load_table_part(k):
+            cols = slice(CUTS[k], CUTS[k + 1])
+            nc.sync.dma_start(out=words[0][:, cols], in_=tab[:, cols])
+
+        def load_weight_scales(w):
+            nc.sync.dma_start(out=s_raw[w // 2][0:P:8, w % 2, :], in_=s_src[w][0].bitcast(I32))
+
         nc.sync.dma_start(lists[0][:], offs)
         nc.sync.dma_start(lists[1][:], offs2)
-        for w in range(2):
-            w_raw[w] = keep.tile([P, R // 2], I32, name=f"w_raw{w}", align_bytes=64)
-            nc.sync.dma_start(out=w_raw[w][:], in_=w_src[w][0].bitcast(I32))
-        tab = tab_words[0].rearrange("p t i -> p (t i)").bitcast(I32)
-        nc.sync.dma_start(out=words[0][:, :LEAD], in_=tab[:, :LEAD])
-        for i, src in enumerate((tab_scales, tab2_scales)):
-            nc.sync.dma_start(out=wins[i][0:P:8, :].bitcast(I32), in_=src[0].bitcast(I32))
-        nc.sync.dma_start(out=words[0][:, LEAD:], in_=tab[:, LEAD:])
-        for i, src in enumerate((wer_scales, wei_scales, wrr_scales, wri_scales)):
-            nc.sync.dma_start(out=s_raw[0:P:8, i, :], in_=src[0].bitcast(I32))
-        nc.sync.dma_start(out=words[1][:], in_=tab2_words[0].rearrange("p t i -> p (t i)").bitcast(I32))
+        load_weight(0)
+        load_weight(1)
+        load_table_part(0)
+        nc.sync.dma_start(out=wins[0][0:P:8, :].bitcast(I32), in_=tab_scales[0].bitcast(I32))
+        load_table_part(1)
+        load_weight_scales(0)
+        load_weight_scales(1)
+        nc.sync.dma_start(out=wins[1][0:P:8, :].bitcast(I32), in_=tab2_scales[0].bitcast(I32))
+        load_table_part(2)
+        load_weight_scales(2)
+        load_weight_scales(3)
+        load_weight(2, PICK_AT[2])
 
         g_words = {}
-        picked = big.tile([P, 2 * J], U8, name="picked", align_bytes=64, offset=PICK_AT)
+        cols = HALF // 16
 
         def gather_words(i, h):
-            cols = HALF // 16
-            if i == 0:
-                g_words[i, h] = big.tile([P, HALF], U32, name=f"g_words{i}{h}", align_bytes=64, offset=PICK_AT + (-3 * R, 3 * R)[h])
-            else:
-                g_words[i, h] = keep.tile([P, HALF], U32, name=f"g_words{i}{h}", align_bytes=64)
+            g_words[i, h] = keep.tile([P, HALF], U32, name=f"g_words{i}{h}", align_bytes=64)
             nc.vector.tensor_copy(g_words[i, h][:], words[i][:].bitcast(U32).indirect(lists[i][:, h * cols : (h + 1) * cols]))
 
-        for i in range(2):
-            nc.vector.tensor_copy(picked[:, i * J : (i + 1) * J], wins[i][:].indirect(lists[i][:]))
-        nc.gpsimd.tensor_copy(plane[:, 0 : 4 * R].bitcast(I32).rearrange("p (w t m) -> p w t m", w=4, t=PACK),
-                              s_raw[:].rearrange("p w (m t) -> p w t m", t=PACK))
-        nc.vector.tensor_copy(plane[:, 4 * R :].bitcast(I32), picked[:].bitcast(I32))
-        for r in range(1, 4):
-            nc.scalar.dma_start(out=plane[r:P:32, :].bitcast(I32), in_=plane[8 * r : P : 32, :].bitcast(I32))
-        for i, w in enumerate((2, 3)):
-            w_raw[w] = big.tile([P, R // 2], I32, name=f"w_raw{w}", align_bytes=64, offset=(PICK_AT + R, S_AT + R)[i])
-            (nc.sync, nc.scalar)[i].dma_start(out=w_raw[w][:], in_=w_src[w][0].bitcast(I32))
+        def deal_words(w):
+            w_words[w] = keep.tile([P, PACK, P // 2], U32, name=f"w_words{w}", align_bytes=64)
+            copy = nc.gpsimd.tensor_copy if w == 3 else nc.scalar.copy
+            copy(w_words[w][:].rearrange("p t (m k) -> p t m k", k=2),
+                 w_raw[w][:].bitcast(U32).rearrange("p (m t k) -> p t m k", t=PACK, k=2))
 
-        def deal_words(w, engine):
-            w_words[w] = keep.tile([P, PACK, P // 2], I32, name=f"w_words{w}", align_bytes=64)
-            engine.tensor_copy(w_words[w][:].rearrange("p t (m k) -> p t m k", k=2),
-                               w_raw[w][:].rearrange("p (m t k) -> p t m k", t=PACK, k=2))
+        def fill_plane(g):
+            W = len(PICKS[g]) * HALF
+            picked = big.tile([P, W], U8, name=f"picked{g}", align_bytes=64, offset=PICK_AT[g])
+            for k, (i, h) in enumerate(PICKS[g]):
+                nc.vector.tensor_copy(picked[:, k * HALF : (k + 1) * HALF], wins[i][:].indirect(lists[i][:, h * cols : (h + 1) * cols]))
+            nc.vector.tensor_copy(planes[g][:, 0:W].bitcast(I32), picked[:].bitcast(I32))
+            if g < 2:
+                nc.scalar.copy(planes[g][:, W:].bitcast(U32).rearrange("p (w t m) -> p w t m", w=2, t=PACK),
+                               s_raw[g][:].bitcast(U32).rearrange("p w (m t) -> p w t m", t=PACK))
+            for r in range(1, 4):
+                nc.sync.dma_start(out=planes[g][r:P:32, :].bitcast(I32), in_=planes[g][8 * r : P : 32, :].bitcast(I32))
 
-        deal_words(0, nc.vector)
-        deal_words(1, nc.vector)
+        deal_words(0)
+        deal_words(1)
+        fill_plane(0)
+        nc.sync.dma_start(out=words[1][:], in_=tab2_words[0].rearrange("p t i -> p (t i)").bitcast(I32))
+        load_weight(3, W3_AT)
+        fill_plane(1)
         gather_words(0, 0)
+        deal_words(2)
+        fill_plane(2)
         gather_words(0, 1)
-        warm = psum.tile([P, HALF], F32, name="warm", offset=7 * BANK)
-        for rep in range(4):
-            nc.tensor.matmul_mx(out=warm[:], lhsT=g_words[0, 0][:, rep * P : (rep + 1) * P].bitcast(FP8X4), lhsT_scale=wins[0][:, 0:P],
-                                rhs=w_words[0][:].rearrange("p t m -> p (t m)").bitcast(U8).bitcast(FP4X4), rhs_scale=wins[0][:, 0:R], start=True, stop=True)
         gather_words(1, 0)
-        deal_words(2, nc.gpsimd)
         gather_words(1, 1)
-        deal_words(3, nc.gpsimd)
+        deal_words(3)
         n_raw = [big.tile([P, PACK, N], F32, name=f"n_raw{i}", align_bytes=64, offset=16 * N * i) for i in range(2)]
         for c, src in enumerate((nr, ni)):
             for i in range(4):
@@ -115,28 +136,37 @@ def tile_list_ckg_none_kernel(tc, tab_words, tab_scales, tab2_words, tab2_scales
             tb = w // 2
             bank = psum.tile([P, PACK, P], F32, name=f"a{w}_{jt}", offset=b * BANK)
             h, c = divmod(jt * P, HALF)
-            s0 = 4 * R + tb * J + jt * P
+            g, k = PICK_PLACE[tb, h]
+            s0 = k * HALF + c
+            w0 = HALF + w % 2 * R
             if jt in TURNED:
                 nc.tensor.matmul_mx(out=bank[:].rearrange("j t p -> j (t p)"),
-                                    lhsT=g_words[tb, h][:, c : c + P].bitcast(FP8X4), lhsT_scale=plane[:, s0 : s0 + P],
+                                    lhsT=g_words[tb, h][:, c : c + P].bitcast(FP8X4), lhsT_scale=planes[g][:, s0 : s0 + P],
                                     rhs=w_words[w][:].rearrange("p t m -> p (t m)").bitcast(U8).bitcast(FP4X4),
-                                    rhs_scale=plane[:, w * R : (w + 1) * R], start=True, stop=True)
+                                    rhs_scale=planes[tb][:, w0 : w0 + R], start=True, stop=True)
                 return bank[:].rearrange("j t p -> j (t p)").rearrange("j (a b) -> j a b", b=PACK)
             for t in range(PACK):
                 nc.tensor.matmul_mx(out=bank[:, t, :], lhsT=w_words[w][:, t, :].bitcast(U8).bitcast(FP4X4),
-                                    lhsT_scale=plane[:, w * R + t * P : w * R + (t + 1) * P],
-                                    rhs=g_words[tb, h][:, c : c + P].bitcast(FP8X4), rhs_scale=plane[:, s0 : s0 + P],
+                                    lhsT_scale=planes[tb][:, w0 + t * P : w0 + (t + 1) * P],
+                                    rhs=g_words[tb, h][:, c : c + P].bitcast(FP8X4), rhs_scale=planes[g][:, s0 : s0 + P],
                                     start=True, stop=True)
             return bank[:].rearrange("p t j -> p j t")
 
-        ent, arr_sb, rel, pa, pb, h_bf, h_q = {}, {}, {}, {}, {}, {}, {}
+        ent, ent_bank, arr_sb, rel, pa, pb, h_bf, h_q = {}, {}, {}, {}, {}, {}, {}, {}
 
-        def entity(jt, c, b):
+        def fill_entity(jt, c, b):
+            ent_bank[jt, c] = project(c, jt, b)
+
+        def copy_entity(jt, c):
             if (jt, c) == (6, 0):
                 ent[jt] = big.tile([P, 2, P, PACK], F32, name="ent6", offset=ENT6_AT)
             elif c == 0:
                 ent[jt] = keep.tile([P, 2, P, PACK], F32, name=f"ent{jt}")
-            nc.scalar.copy(ent[jt][:, c], project(c, jt, b))
+            nc.scalar.copy(ent[jt][:, c], ent_bank[jt, c])
+
+        def entity(jt, c, b):
+            fill_entity(jt, c, b)
+            copy_entity(jt, c)
 
         def arr_out(jt, b):
             arr_sb[jt] = keep.tile([P, P, PACK], F32, name=f"arr{jt}")
@@ -146,7 +176,7 @@ def tile_list_ckg_none_kernel(tc, tab_words, tab_scales, tab2_words, tab2_scales
             rel[jt, c] = project(2 + c, jt, b)
 
         def prod_tile(name, jt, s):
-            if jt == 4:
+            if jt == 2:
                 return big.tile([P, 2, P, PACK], F32, name=name, offset=PROD4_AT + 4 * KB * s)
             return keep.tile([P, 2, P, PACK], F32, name=name)
 
@@ -262,79 +292,81 @@ def tile_list_ckg_none_kernel(tc, tab_words, tab_scales, tab2_words, tab2_scales
                 (nc.scalar, nc.sync)[nt].dma_start(out=out[nt * P : (nt + 1) * P, J - P :], in_=y[:])
 
         entity(0, 0, 4)
-        relation(0, 0, 0)
         entity(0, 1, 5)
-        relation(0, 1, 1)
         entity(1, 0, 6)
-        relation(1, 0, 2)
         entity(1, 1, 7)
-        relation(1, 1, 3)
-        for jt in range(2):
-            times_arr(jt, 0)
-            times_ari(jt, 0)
-            add_on_gpsimd(jt, 0)
-            times_arr(jt, 1)
-            relation(2 + jt, jt, 2 * jt)
-            times_ari(jt, 1)
-            add_on_gpsimd(jt, 1)
-            if jt == 0:
-                relation(2, 1, 1)
-                entity(2, 0, 4)
-                entity(2, 1, 5)
-                entity(3, 0, 6)
-                entity(3, 1, 7)
-        arr_out(3, 3)
-        times_arr(3)
-        times_arr(2)
-        relation(4, 0, 0)
-        entity(4, 0, 4)
-        entity(4, 1, 5)
-        times_ari(2)
-        relation(4, 1, 1)
-        entity(5, 0, 4)
-        entity(5, 1, 5)
-        arr_out(5, 3)
-        times_arr(5)
-        times_ari(3)
-        relation(5, 1, 2)
-        times_arr(4)
-        relation(6, 0, 0)
+        entity(2, 0, 2)
+        entity(2, 1, 3)
+        fill_entity(3, 0, 4)
+        fill_entity(3, 1, 5)
+        relation(0, 0, 0)
+        arr_out(1, 6)
+        relation(0, 1, 1)
+        copy_entity(3, 0)
+        copy_entity(3, 1)
+        arr_out(3, 7)
+        relation(1, 1, 2)
+        relation(2, 0, 3)
+        entity(4, 0, 6)
+        entity(4, 1, 4)
+        times_arr(1)
+        times_arr(0)
+        relation(2, 1, 0)
+        arr_out(4, 5)
+        entity(5, 0, 7)
+        times_ari(0)
+        relation(3, 1, 1)
+        entity(5, 1, 6)
         entity(6, 0, 4)
+        times_arr(3)
+        times_ari(1)
+        relation(4, 1, 2)
         entity(6, 1, 5)
-        turn(2, 0, 6)
-        turn(2, 1, 7)
-        times_ari(4)
-        add_on_gpsimd(4)
-        relation(6, 1, 1)
-        relation(7, 1, 3)
+        turn(1, 0, 7)
+        turn(1, 1, 6)
+        times_arr(2)
+        relation(5, 0, 3)
         entity(7, 0, 4)
         entity(7, 1, 5)
+        times_arr(4)
+        times_ari(2)
+        relation(5, 1, 0)
+        times_ari(3)
+        relation(6, 0, 1)
         cast_n(0)
-        cast_n(1)
-        turn(3, 0, 6)
-        turn(3, 1, 7)
+        turn(3, 0, 7)
+        turn(3, 1, 6)
+        times_ari(4)
+        relation(6, 1, 2)
+        add_on_gpsimd(0)
+        times_arr(5)
+        relation(7, 0, 3)
+        turn(4, 0, 4)
+        turn(4, 1, 5)
         times_ari(5)
-        relation(7, 0, 2)
-        turn(5, 0, 4)
-        turn(5, 1, 5)
+        relation(7, 1, 0)
+        add_on_gpsimd(2)
+        cast_n(1)
+        turn(5, 0, 7)
+        turn(5, 1, 6)
         times_arr(6)
         times_ari(6)
-        turn(6, 0, 6)
-        turn(6, 1, 7)
+        turn(6, 0, 4)
+        turn(6, 1, 5)
         times_arr(7)
         quantise_n()
         quantise(0)
-        score(0, 0)
+        score(0, 1)
         times_ari(7, 0)
         quantise(1)
-        score(1, 1)
+        score(1, 2)
         times_ari(7, 1)
         quantise(2)
-        score(2, 2)
+        score(2, 7)
         quantise(3)
-        score(3, 4)
+        score(3, 6)
         add_on_vector(7, 0)
         add_on_vector(7, 1)
         quantise(4, 0)
         quantise(4, 1)
-        score_last(0, 5)
+        score_last(1, 4)

@@ -29,6 +29,7 @@ TURNED = (1, 3, 4, 5, 6)
 SHARED = (1, 3, 4)
 GROUPS = ((0, 1), (2, 3), (4, 5), (6,), (7,))
 GROUP_OF = {jt: g for g, tiles in enumerate(GROUPS) for jt in tiles}
+H6_AT = 68 * KB
 TAB_AT, W3_AT = (0, 20 * KB), 19 * KB - 256
 WIN_AT, PICK_AT, S_AT, PROD4_AT, H23_AT, ENT6_AT = 38 * KB, (36 * KB - 256, 36 * KB, 36 * KB + 512), (20 * KB - 512, 46 * KB), 48 * KB, 56 * KB, 60 * KB
 
@@ -97,9 +98,8 @@ def tile_list_ckg_none_kernel(tc, tab_words, tab_scales, tab2_words, tab2_scales
 
         def deal_words(w):
             w_words[w] = keep.tile([P, PACK, P // 2], U32, name=f"w_words{w}", align_bytes=64)
-            copy = nc.gpsimd.tensor_copy if w == 3 else nc.scalar.copy
-            copy(w_words[w][:].rearrange("p t (m k) -> p t m k", k=2),
-                 w_raw[w][:].bitcast(U32).rearrange("p (m t k) -> p t m k", t=PACK, k=2))
+            nc.scalar.copy(w_words[w][:].rearrange("p t (m k) -> p t m k", k=2),
+                           w_raw[w][:].bitcast(U32).rearrange("p (m t k) -> p t m k", t=PACK, k=2))
 
         def fill_plane(g):
             W = len(PICKS[g]) * HALF
@@ -125,7 +125,6 @@ def tile_list_ckg_none_kernel(tc, tab_words, tab_scales, tab2_words, tab2_scales
         gather_words(0, 1)
         gather_words(1, 0)
         gather_words(1, 1)
-        deal_words(3)
         n_raw = [big.tile([P, PACK, N], F32, name=f"n_raw{i}", align_bytes=64, offset=16 * N * i) for i in range(2)]
         for c, src in enumerate((nr, ni)):
             for i in range(4):
@@ -158,8 +157,8 @@ def tile_list_ckg_none_kernel(tc, tab_words, tab_scales, tab2_words, tab2_scales
             ent_bank[jt, c] = project(c, jt, b)
 
         def copy_entity(jt, c):
-            if (jt, c) == (6, 0):
-                ent[jt] = big.tile([P, 2, P, PACK], F32, name="ent6", offset=ENT6_AT)
+            if c == 0 and jt >= 6:
+                ent[jt] = big.tile([P, 2, P, PACK], F32, name=f"ent{jt}", offset=ENT6_AT + (jt - 6) * 4 * KB)
             elif c == 0:
                 ent[jt] = keep.tile([P, 2, P, PACK], F32, name=f"ent{jt}")
             nc.scalar.copy(ent[jt][:, c], ent_bank[jt, c])
@@ -178,6 +177,8 @@ def tile_list_ckg_none_kernel(tc, tab_words, tab_scales, tab2_words, tab2_scales
         def prod_tile(name, jt, s):
             if jt == 2:
                 return big.tile([P, 2, P, PACK], F32, name=name, offset=PROD4_AT + 4 * KB * s)
+            if (jt, s) == (7, 1):
+                return big.tile([P, 2, P, PACK], F32, name=name, offset=H23_AT)
             return keep.tile([P, 2, P, PACK], F32, name=name)
 
         def times_arr(jt, c=None):
@@ -202,8 +203,8 @@ def tile_list_ckg_none_kernel(tc, tab_words, tab_scales, tab2_words, tab2_scales
             g = GROUP_OF[jt]
             if g not in h_bf:
                 shape = [P, 2, len(GROUPS[g]) * P, PACK]
-                if g == 1:
-                    h_bf[g] = big.tile(shape, BF16, name=f"h_bf{g}", align_bytes=64, offset=H23_AT)
+                if g >= 2:
+                    h_bf[g] = big.tile(shape, BF16, name=f"h_bf{g}", align_bytes=64, offset=(H23_AT, H6_AT, H6_AT)[g - 2])
                 else:
                     h_bf[g] = keep.tile(shape, BF16, name=f"h_bf{g}", align_bytes=64)
             jj = jt - GROUPS[g][0]
@@ -236,8 +237,8 @@ def tile_list_ckg_none_kernel(tc, tab_words, tab_scales, tab2_words, tab2_scales
                     codes = big.tile([P, 2, W], U32, name="h_codes0", align_bytes=64, offset=PROD4_AT + 4 * KB)
                 else:
                     codes = keep.tile([P, 2, W], U32, name=f"h_codes{g}", align_bytes=64)
-                if g < 2:
-                    scales = big.tile([P, 2, W], U8, name=f"h_plane{g}", align_bytes=64, offset=ENT6_AT + (g + 1) * KB)
+                if g < 4:
+                    scales = big.tile([P, 2, W], U8, name=f"h_plane{g}", align_bytes=64, offset=ENT6_AT + (1, 2, 3, 5)[g] * KB)
                 else:
                     scales = keep.tile([P, 2, W], U8, name=f"h_plane{g}", align_bytes=64)
                 h_q[g] = (codes, scales)
@@ -294,36 +295,35 @@ def tile_list_ckg_none_kernel(tc, tab_words, tab_scales, tab2_words, tab2_scales
         entity(0, 0, 4)
         entity(0, 1, 5)
         entity(1, 0, 6)
-        entity(1, 1, 7)
-        entity(2, 0, 2)
-        entity(2, 1, 3)
-        fill_entity(3, 0, 4)
-        fill_entity(3, 1, 5)
+        entity(1, 1, 4)
+        entity(2, 0, 5)
+        entity(2, 1, 6)
+        entity(3, 0, 4)
+        entity(3, 1, 5)
+        deal_words(3)
+        arr_out(1, 7)
         relation(0, 0, 0)
-        arr_out(1, 6)
         relation(0, 1, 1)
-        copy_entity(3, 0)
-        copy_entity(3, 1)
-        arr_out(3, 7)
+        arr_out(3, 6)
         relation(1, 1, 2)
         relation(2, 0, 3)
-        entity(4, 0, 6)
+        entity(4, 0, 7)
         entity(4, 1, 4)
         times_arr(1)
         times_arr(0)
         relation(2, 1, 0)
         arr_out(4, 5)
-        entity(5, 0, 7)
+        entity(5, 0, 6)
         times_ari(0)
         relation(3, 1, 1)
-        entity(5, 1, 6)
+        entity(5, 1, 7)
         entity(6, 0, 4)
         times_arr(3)
         times_ari(1)
         relation(4, 1, 2)
         entity(6, 1, 5)
-        turn(1, 0, 7)
-        turn(1, 1, 6)
+        turn(1, 0, 6)
+        turn(1, 1, 7)
         times_arr(2)
         relation(5, 0, 3)
         entity(7, 0, 4)
@@ -334,8 +334,8 @@ def tile_list_ckg_none_kernel(tc, tab_words, tab_scales, tab2_words, tab2_scales
         times_ari(3)
         relation(6, 0, 1)
         cast_n(0)
-        turn(3, 0, 7)
-        turn(3, 1, 6)
+        turn(3, 0, 6)
+        turn(3, 1, 7)
         times_ari(4)
         relation(6, 1, 2)
         add_on_gpsimd(0)
@@ -347,8 +347,8 @@ def tile_list_ckg_none_kernel(tc, tab_words, tab_scales, tab2_words, tab2_scales
         relation(7, 1, 0)
         add_on_gpsimd(2)
         cast_n(1)
-        turn(5, 0, 7)
-        turn(5, 1, 6)
+        turn(5, 0, 6)
+        turn(5, 1, 7)
         times_arr(6)
         times_ari(6)
         turn(6, 0, 4)
@@ -357,14 +357,13 @@ def tile_list_ckg_none_kernel(tc, tab_words, tab_scales, tab2_words, tab2_scales
         quantise_n()
         quantise(0)
         score(0, 1)
-        times_ari(7, 0)
         quantise(1)
         score(1, 2)
-        times_ari(7, 1)
         quantise(2)
-        score(2, 7)
+        score(2, 6)
+        times_ari(7)
         quantise(3)
-        score(3, 6)
+        score(3, 7)
         add_on_vector(7, 0)
         add_on_vector(7, 1)
         quantise(4, 0)

@@ -111,7 +111,8 @@ def tile_list_ckg_none_kernel(tc, tab_words, tab_scales, tab2_words, tab2_scales
                 nc.scalar.copy(planes[g][:, W:].bitcast(U32).rearrange("p (w t m) -> p w t m", w=2, t=PACK),
                                s_raw[g][:].bitcast(U32).rearrange("p w (m t) -> p w t m", t=PACK))
             for r in range(1, 4):
-                nc.sync.dma_start(out=planes[g][r:P:32, :].bitcast(I32), in_=planes[g][8 * r : P : 32, :].bitcast(I32))
+                queue = nc.scalar if g == 1 else nc.sync
+                queue.dma_start(out=planes[g][r:P:32, :].bitcast(I32), in_=planes[g][8 * r : P : 32, :].bitcast(I32))
 
         deal_words(0)
         deal_words(1)

@@ -178,8 +178,6 @@ def tile_list_ckg_none_kernel(tc, tab_words, tab_scales, tab2_words, tab2_scales
         def prod_tile(name, jt, s):
             if jt == 2:
                 return big.tile([P, 2, P, PACK], F32, name=name, offset=PROD4_AT + 4 * KB * s)
-            if (jt, s) == (7, 1):
-                return big.tile([P, 2, P, PACK], F32, name=name, offset=H23_AT)
             return keep.tile([P, 2, P, PACK], F32, name=name)
 
         def times_arr(jt, c=None):
@@ -205,7 +203,7 @@ def tile_list_ckg_none_kernel(tc, tab_words, tab_scales, tab2_words, tab2_scales
             if g not in h_bf:
                 shape = [P, 2, len(GROUPS[g]) * P, PACK]
                 if g >= 2:
-                    h_bf[g] = big.tile(shape, BF16, name=f"h_bf{g}", align_bytes=64, offset=(H23_AT, H6_AT, H6_AT)[g - 2])
+                    h_bf[g] = big.tile(shape, BF16, name=f"h_bf{g}", align_bytes=64, offset=(H23_AT, H6_AT, H23_AT)[g - 2])
                 else:
                     h_bf[g] = keep.tile(shape, BF16, name=f"h_bf{g}", align_bytes=64)
             jj = jt - GROUPS[g][0]
@@ -238,8 +236,10 @@ def tile_list_ckg_none_kernel(tc, tab_words, tab_scales, tab2_words, tab2_scales
                     codes = big.tile([P, 2, W], U32, name="h_codes0", align_bytes=64, offset=PROD4_AT + 4 * KB)
                 else:
                     codes = keep.tile([P, 2, W], U32, name=f"h_codes{g}", align_bytes=64)
-                if g < 4:
-                    scales = big.tile([P, 2, W], U8, name=f"h_plane{g}", align_bytes=64, offset=ENT6_AT + (1, 2, 3, 5)[g] * KB)
+                if g == 4:
+                    scales = big.tile([P, 2, W], U8, name=f"h_plane{g}", align_bytes=64, offset=H6_AT)
+                elif g < 3:
+                    scales = big.tile([P, 2, W], U8, name=f"h_plane{g}", align_bytes=64, offset=ENT6_AT + (g + 1) * KB)
                 else:
                     scales = keep.tile([P, 2, W], U8, name=f"h_plane{g}", align_bytes=64)
                 h_q[g] = (codes, scales)
@@ -323,6 +323,7 @@ def tile_list_ckg_none_kernel(tc, tab_words, tab_scales, tab2_words, tab2_scales
         times_ari(1)
         relation(4, 1, 2)
         entity(6, 1, 5)
+        cast_n(0)
         turn(1, 0, 6)
         turn(1, 1, 7)
         times_arr(2)
@@ -334,7 +335,7 @@ def tile_list_ckg_none_kernel(tc, tab_words, tab_scales, tab2_words, tab2_scales
         relation(5, 1, 0)
         times_ari(3)
         relation(6, 0, 1)
-        cast_n(0)
+        cast_n(1)
         turn(3, 0, 6)
         turn(3, 1, 7)
         times_ari(4)
@@ -347,7 +348,6 @@ def tile_list_ckg_none_kernel(tc, tab_words, tab_scales, tab2_words, tab2_scales
         times_ari(5)
         relation(7, 1, 0)
         add_on_gpsimd(2)
-        cast_n(1)
         turn(5, 0, 6)
         turn(5, 1, 7)
         times_arr(6)
@@ -360,12 +360,13 @@ def tile_list_ckg_none_kernel(tc, tab_words, tab_scales, tab2_words, tab2_scales
         score(0, 1)
         quantise(1)
         score(1, 2)
+        times_ari(7, 0)
         quantise(2)
         score(2, 6)
-        times_ari(7)
+        times_ari(7, 1)
+        add_on_vector(7, 0)
         quantise(3)
         score(3, 7)
-        add_on_vector(7, 0)
         add_on_vector(7, 1)
         quantise(4, 0)
         quantise(4, 1)

@@ -236,9 +236,7 @@ def tile_list_ckg_none_kernel(tc, tab_words, tab_scales, tab2_words, tab2_scales
                     codes = big.tile([P, 2, W], U32, name="h_codes0", align_bytes=64, offset=PROD4_AT + 4 * KB)
                 else:
                     codes = keep.tile([P, 2, W], U32, name=f"h_codes{g}", align_bytes=64)
-                if g == 4:
-                    scales = big.tile([P, 2, W], U8, name=f"h_plane{g}", align_bytes=64, offset=H6_AT)
-                elif g < 3:
+                if g < 3:
                     scales = big.tile([P, 2, W], U8, name=f"h_plane{g}", align_bytes=64, offset=ENT6_AT + (g + 1) * KB)
                 else:
                     scales = keep.tile([P, 2, W], U8, name=f"h_plane{g}", align_bytes=64)
@@ -251,6 +249,15 @@ def tile_list_ckg_none_kernel(tc, tab_words, tab_scales, tab2_words, tab2_scales
             else:
                 nc.vector.quantize_mx(out=codes[:, c, :].bitcast(FP8X4), scales=scales[:, c, :],
                                       in_=h_bf[g][:, c].rearrange("p j t -> p (j t)"))
+
+        def quantise_last(jt, c):
+            if 3 not in h_q:
+                h_q[3] = (keep.tile([P, 2, 2 * P], U32, name="h_codes3", align_bytes=64),
+                          keep.tile([P, 2, 2 * P], U8, name="h_plane3", align_bytes=64))
+            codes, scales = h_q[3]
+            cols = slice((jt - 6) * P, (jt - 5) * P)
+            nc.vector.quantize_mx(out=codes[:, c, cols].bitcast(FP8X4), scales=scales[:, c, cols],
+                                  in_=h_slot(jt)[:, c].rearrange("p j t -> p (j t)"))
 
         def add_on_vector(jt, c):
             nc.vector.tensor_tensor(h_slot(jt)[:, c], pa[jt][:, c], pb[jt][:, c], ADD)
@@ -281,17 +288,17 @@ def tile_list_ckg_none_kernel(tc, tab_words, tab_scales, tab2_words, tab2_scales
             nc.sync.dma_start(out=out.rearrange("(nt p) j -> p nt j", p=P)[:, :, j0 : j0 + W], in_=y[:])
 
         def score_last(b0, b1):
-            banks = [psum.tile([P, P], F32, name=f"y_last{nt}", offset=(b0, b1)[nt] * BANK) for nt in range(2)]
+            banks = [psum.tile([P, 2 * P], F32, name=f"y_last{nt}", offset=(b0, b1)[nt] * BANK) for nt in range(2)]
             for c in range(2):
                 for nt in range(2):
-                    score_pass(banks[nt][:], len(GROUPS) - 1, c, nt, c == 0, c == 1)
+                    score_pass(banks[nt][:], 3, c, nt, c == 0, c == 1)
             for nt in range(2):
-                y = keep.tile([P, P], F32, name=f"y_last_sb{nt}")
+                y = keep.tile([P, 2 * P], F32, name=f"y_last_sb{nt}")
                 if nt == 0:
                     nc.scalar.copy(y[:], banks[nt][:])
                 else:
                     nc.vector.tensor_copy(y[:], banks[nt][:])
-                (nc.scalar, nc.sync)[nt].dma_start(out=out[nt * P : (nt + 1) * P, J - P :], in_=y[:])
+                (nc.scalar, nc.sync)[nt].dma_start(out=out[nt * P : (nt + 1) * P, J - 2 * P :], in_=y[:])
 
         entity(0, 0, 4)
         entity(0, 1, 5)
@@ -365,9 +372,9 @@ def tile_list_ckg_none_kernel(tc, tab_words, tab_scales, tab2_words, tab2_scales
         score(2, 6)
         times_ari(7, 1)
         add_on_vector(7, 0)
-        quantise(3)
-        score(3, 7)
+        quantise_last(6, 0)
+        quantise_last(6, 1)
         add_on_vector(7, 1)
-        quantise(4, 0)
-        quantise(4, 1)
+        quantise_last(7, 0)
+        quantise_last(7, 1)
         score_last(1, 4)

from contextlib import ExitStack

import concourse.mybir as mybir
from concourse.masks import make_identity

K, L, R, N, T, J = 512, 512, 512, 256, 4096, 1024
FLOPS = 2 * 4 * K * R * J + 2 * 2 * R * N * J

F32 = mybir.dt.float32
BF16 = mybir.dt.bfloat16
I32 = mybir.dt.int32
U32 = mybir.dt.uint32
U16 = mybir.dt.uint16
U8 = mybir.dt.uint8
FP8X4 = mybir.dt.float8_e4m3fn_x4
FP4X4 = mybir.dt.float4_e2m1fn_x4
MULT = mybir.AluOpType.mult
ADD = mybir.AluOpType.add

P = 128
PACK = 4
HALF = J // 2
KB = 1024
BANK = 2 * KB
CUTS = (0, T // 8, 3 * T // 8, T)
PICKS = (((0, 0),), ((1, 0),), ((0, 1), (1, 1)))
PICK_PLACE = {key: (g, k) for g, keys in enumerate(PICKS) for k, key in enumerate(keys)}
TURNED = (1, 3, 4, 5, 6)
SHARED = (1, 3, 4)
GROUPS = ((0, 1), (2, 3), (4, 5), (6,), (7,))
GROUP_OF = {jt: g for g, tiles in enumerate(GROUPS) for jt in tiles}
H6_AT = 68 * KB
TAB_AT, W3_AT = (0, 20 * KB), 19 * KB - 256
WIN_AT, PICK_AT, S_AT, PROD4_AT, H23_AT, ENT6_AT = 38 * KB, (36 * KB - 256, 36 * KB, 36 * KB + 512), (20 * KB - 512, 46 * KB), 48 * KB, 56 * KB, 60 * KB


def tile_list_ckg_none_kernel(tc, tab_words, tab_scales, tab2_words, tab2_scales, wer_words, wer_scales, wei_words,
        wei_scales, wrr_words, wrr_scales, wri_words, wri_scales, nr, ni, offs, offs2, out):
    nc = tc.nc
    with ExitStack() as ctx:
        keep = ctx.enter_context(tc.tile_pool(name="keep", bufs=1))
        big = ctx.enter_context(tc.tile_pool(name="big", bufs=1))
        psum = ctx.enter_context(tc.psum_pool(name="psum", bufs=1))

        lists = [keep.tile([P, J // 16], U16, name=f"list{i}") for i in range(2)]
        words = [big.tile([P, T], I32, name=f"words{i}", align_bytes=64, offset=TAB_AT[i]) for i in range(2)]
        wins = [big.tile([P, T], U8, name=f"win{i}", align_bytes=64, offset=WIN_AT + T * i) for i in range(2)]
        s_raw = [big.tile([P, 2, R // 4], I32, name=f"s_raw{g}", align_bytes=64, offset=S_AT[g]) for g in range(2)]
        planes = [keep.tile([P, (HALF + 2 * R, HALF + 2 * R, J)[g]], U8, name=f"plane{g}", align_bytes=64) for g in range(3)]

        nc.gpsimd.memset(wins[0][:].bitcast(I32), 0)
        for g in range(2):
            nc.vector.memset(s_raw[g][:], 0)
        nc.vector.memset(wins[1][:].bitcast(I32), 0)
        ident = keep.tile([P, P], F32, name="ident")
        make_identity(nc, ident[:])

        w_src = (wer_words, wei_words, wrr_words, wri_words)
        s_src = (wer_scales, wei_scales, wrr_scales, wri_scales)
        w_raw, w_words = {}, {}
        tab = tab_words[0].rearrange("p t i -> p (t i)").bitcast(I32)

        def load_weight(w, at=None):
            if at is None:
                w_raw[w] = keep.tile([P, R // 2], I32, name=f"w_raw{w}", align_bytes=64)
            else:
                w_raw[w] = big.tile([P, R // 2], I32, name=f"w_raw{w}", align_bytes=64, offset=at)
            nc.sync.dma_start(out=w_raw[w][:], in_=w_src[w][0].bitcast(I32))

        def load_table_part(k):
            cols = slice(CUTS[k], CUTS[k + 1])
            nc.sync.dma_start(out=words[0][:, cols], in_=tab[:, cols])

        def load_weight_scales(w):
            nc.sync.dma_start(out=s_raw[w // 2][0:P:8, w % 2, :], in_=s_src[w][0].bitcast(I32))

        nc.sync.dma_start(lists[0][:], offs)
        nc.sync.dma_start(lists[1][:], offs2)
        load_weight(0)
        load_weight(1)
        load_table_part(0)
        nc.sync.dma_start(out=wins[0][0:P:8, :].bitcast(I32), in_=tab_scales[0].bitcast(I32))
        load_table_part(1)
        load_weight_scales(0)
        load_weight_scales(1)
        nc.sync.dma_start(out=wins[1][0:P:8, :].bitcast(I32), in_=tab2_scales[0].bitcast(I32))
        load_table_part(2)
        load_weight_scales(2)
        load_weight_scales(3)
        load_weight(2, PICK_AT[2])

        g_words = {}
        cols = HALF // 16

        def gather_words(i, h):
            g_words[i, h] = keep.tile([P, HALF], U32, name=f"g_words{i}{h}", align_bytes=64)
            nc.vector.tensor_copy(g_words[i, h][:], words[i][:].bitcast(U32).indirect(lists[i][:, h * cols : (h + 1) * cols]))

        def deal_words(w):
            w_words[w] = keep.tile([P, PACK, P // 2], U32, name=f"w_words{w}", align_bytes=64)
            nc.scalar.copy(w_words[w][:].rearrange("p t (m k) -> p t m k", k=2),
                           w_raw[w][:].bitcast(U32).rearrange("p (m t k) -> p t m k", t=PACK, k=2))

        def fill_plane(g):
            W = len(PICKS[g]) * HALF
            picked = big.tile([P, W], U8, name=f"picked{g}", align_bytes=64, offset=PICK_AT[g])
            for k, (i, h) in enumerate(PICKS[g]):
                nc.vector.tensor_copy(picked[:, k * HALF : (k + 1) * HALF], wins[i][:].indirect(lists[i][:, h * cols : (h + 1) * cols]))
            nc.vector.tensor_copy(planes[g][:, 0:W].bitcast(I32), picked[:].bitcast(I32))
            if g < 2:
                nc.scalar.copy(planes[g][:, W:].bitcast(U32).rearrange("p (w t m) -> p w t m", w=2, t=PACK),
                               s_raw[g][:].bitcast(U32).rearrange("p w (m t) -> p w t m", t=PACK))
            for r in range(1, 4):
                queue = nc.scalar if g == 1 else nc.sync
                queue.dma_start(out=planes[g][r:P:32, :].bitcast(I32), in_=planes[g][8 * r : P : 32, :].bitcast(I32))

        deal_words(0)
        deal_words(1)
        fill_plane(0)
        nc.sync.dma_start(out=words[1][:], in_=tab2_words[0].rearrange("p t i -> p (t i)").bitcast(I32))
        load_weight(3, W3_AT)
        fill_plane(1)
        gather_words(0, 0)
        deal_words(2)
        fill_plane(2)
        gather_words(0, 1)
        gather_words(1, 0)
        gather_words(1, 1)
        n_raw = [big.tile([P, PACK, N], F32, name=f"n_raw{i}", align_bytes=64, offset=16 * N * i) for i in range(2)]
        for c, src in enumerate((nr, ni)):
            for i in range(4):
                nc.sync.dma_start(out=n_raw[c][i:P:4], in_=src.rearrange("(m t i) n -> i m t n", t=PACK, i=4)[i])
        n_bf = keep.tile([P, 2, N, PACK], BF16, name="n_bf", align_bytes=64)

        def project(w, jt, b):
            tb = w // 2
            bank = psum.tile([P, PACK, P], F32, name=f"a{w}_{jt}", offset=b * BANK)
            h, c = divmod(jt * P, HALF)
            g, k = PICK_PLACE[tb, h]
            s0 = k * HALF + c
            w0 = HALF + w % 2 * R
            if jt in TURNED:
                nc.tensor.matmul_mx(out=bank[:].rearrange("j t p -> j (t p)"),
                                    lhsT=g_words[tb, h][:, c : c + P].bitcast(FP8X4), lhsT_scale=planes[g][:, s0 : s0 + P],
                                    rhs=w_words[w][:].rearrange("p t m -> p (t m)").bitcast(U8).bitcast(FP4X4),
                                    rhs_scale=planes[tb][:, w0 : w0 + R], start=True, stop=True)
                return bank[:].rearrange("j t p -> j (t p)").rearrange("j (a b) -> j a b", b=PACK)
            for t in range(PACK):
                nc.tensor.matmul_mx(out=bank[:, t, :], lhsT=w_words[w][:, t, :].bitcast(U8).bitcast(FP4X4),
                                    lhsT_scale=planes[tb][:, w0 + t * P : w0 + (t + 1) * P],
                                    rhs=g_words[tb, h][:, c : c + P].bitcast(FP8X4), rhs_scale=planes[g][:, s0 : s0 + P],
                                    start=True, stop=True)
            return bank[:].rearrange("p t j -> p j t")

        ent, ent_bank, arr_sb, rel, pa, pb, h_bf, h_q = {}, {}, {}, {}, {}, {}, {}, {}

        def fill_entity(jt, c, b):
            ent_bank[jt, c] = project(c, jt, b)

        def copy_entity(jt, c):
            if c == 0 and jt >= 6:
                ent[jt] = big.tile([P, 2, P, PACK], F32, name=f"ent{jt}", offset=ENT6_AT + (jt - 6) * 4 * KB)
            elif c == 0:
                ent[jt] = keep.tile([P, 2, P, PACK], F32, name=f"ent{jt}")
            nc.scalar.copy(ent[jt][:, c], ent_bank[jt, c])

        def entity(jt, c, b):
            fill_entity(jt, c, b)
            copy_entity(jt, c)

        def arr_out(jt, b):
            arr_sb[jt] = keep.tile([P, P, PACK], F32, name=f"arr{jt}")
            nc.scalar.copy(arr_sb[jt][:], project(2, jt, b))

        def relation(jt, c, b):
            rel[jt, c] = project(2 + c, jt, b)

        def prod_tile(name, jt, s):
            if jt == 2:
                return big.tile([P, 2, P, PACK], F32, name=name, offset=PROD4_AT + 4 * KB * s)
            return keep.tile([P, 2, P, PACK], F32, name=name)

        def times_arr(jt, c=None):
            if jt not in pa:
                pa[jt] = prod_tile(f"pa{jt}", jt, 0)
            if jt in SHARED:
                nc.gpsimd.tensor_tensor(pa[jt][:], arr_sb[jt][:].unsqueeze(1).to_broadcast([P, 2, P, PACK]), ent[jt][:], MULT)
            elif c is None:
                nc.vector.tensor_tensor(pa[jt][:], rel[jt, 0].unsqueeze(1).to_broadcast([P, 2, P, PACK]), ent[jt][:], MULT)
            else:
                nc.vector.tensor_tensor(pa[jt][:, c], rel[jt, 0], ent[jt][:, c], MULT)

        def times_ari(jt, c=None):
            if jt not in pb:
                pb[jt] = prod_tile(f"pb{jt}", jt, 1)
            if c != 1:
                nc.vector.scalar_tensor_tensor(pb[jt][:, 0], rel[jt, 1], -1.0, ent[jt][:, 1], MULT, MULT)
            if c != 0:
                nc.vector.tensor_tensor(pb[jt][:, 1], rel[jt, 1], ent[jt][:, 0], MULT)

        def h_slot(jt):
            g = GROUP_OF[jt]
            if g not in h_bf:
                shape = [P, 2, len(GROUPS[g]) * P, PACK]
                if g >= 2:
                    h_bf[g] = big.tile(shape, BF16, name=f"h_bf{g}", align_bytes=64, offset=(H23_AT, H6_AT, H23_AT)[g - 2])
                else:
                    h_bf[g] = keep.tile(shape, BF16, name=f"h_bf{g}", align_bytes=64)
            jj = jt - GROUPS[g][0]
            return h_bf[g][:, :, jj * P : (jj + 1) * P, :]

        def add_on_gpsimd(jt, c=None):
            if c is None:
                nc.gpsimd.tensor_tensor(h_slot(jt), pa[jt][:], pb[jt][:], ADD)
            else:
                nc.gpsimd.tensor_tensor(h_slot(jt)[:, c], pa[jt][:, c], pb[jt][:, c], ADD)

        def turn(jt, c, b):
            bank = psum.tile([P, PACK, P], F32, name=f"h{c}_{jt}", offset=b * BANK)
            for s, prod in enumerate((pb[jt], pa[jt])):
                src = prod[:, c].rearrange("j a b -> j (a b)")
                for t in range(PACK):
                    nc.tensor.matmul(bank[:, t, :], src[:, t * P : (t + 1) * P], ident[:], is_transpose=True,
                                     start=(s == 0 and t == 0), stop=(s == 1 and t == PACK - 1))
            nc.scalar.copy(h_slot(jt)[:, c], bank[:].rearrange("p t j -> p j t"))

        def cast_n(c):
            for h in range(2):
                cols = slice(h * P, (h + 1) * P)
                nc.scalar.copy(n_bf[:, c, cols, :], n_raw[c][:, :, cols].rearrange("p t n -> p n t"))

        def quantise(g, c=None):
            W = len(GROUPS[g]) * P
            if g not in h_q:
                if g == 0:
                    codes = big.tile([P, 2, W], U32, name="h_codes0", align_bytes=64, offset=PROD4_AT + 4 * KB)
                else:
                    codes = keep.tile([P, 2, W], U32, name=f"h_codes{g}", align_bytes=64)
                if g < 3:
                    scales = big.tile([P, 2, W], U8, name=f"h_plane{g}", align_bytes=64, offset=ENT6_AT + (g + 1) * KB)
                else:
                    scales = keep.tile([P, 2, W], U8, name=f"h_plane{g}", align_bytes=64)
                h_q[g] = (codes, scales)
            codes, scales = h_q[g]
            if c is None:
                nc.vector.quantize_mx(out=codes[:].rearrange("p c j -> p (c j)").bitcast(FP8X4),
                                      scales=scales[:].rearrange("p c j -> p (c j)"),
                                      in_=h_bf[g][:].rearrange("p c j t -> p (c j t)"))
            else:
                nc.vector.quantize_mx(out=codes[:, c, :].bitcast(FP8X4), scales=scales[:, c, :],
                                      in_=h_bf[g][:, c].rearrange("p j t -> p (j t)"))

        def quantise_last(jt, c):
            if 3 not in h_q:
                h_q[3] = (keep.tile([P, 2, 2 * P], U32, name="h_codes3", align_bytes=64),
                          keep.tile([P, 2, 2 * P], U8, name="h_plane3", align_bytes=64))
            codes, scales = h_q[3]
            cols = slice((jt - 6) * P, (jt - 5) * P)
            nc.vector.quantize_mx(out=codes[:, c, cols].bitcast(FP8X4), scales=scales[:, c, cols],
                                  in_=h_slot(jt)[:, c].rearrange("p j t -> p (j t)"))

        def add_on_vector(jt, c):
            nc.vector.tensor_tensor(h_slot(jt)[:, c], pa[jt][:, c], pb[jt][:, c], ADD)

        n_q = []

        def quantise_n():
            codes = big.tile([P, 2 * N], U32, name="n_codes", align_bytes=64, offset=PROD4_AT)
            scales = big.tile([P, 2 * N], U8, name="n_plane", align_bytes=64, offset=ENT6_AT)
            nc.vector.quantize_mx(out=codes[:].bitcast(FP8X4), scales=scales[:], in_=n_bf[:].rearrange("p c n t -> p (c n t)"))
            n_q.extend((codes, scales))

        def score_pass(bank, g, c, nt, start, stop):
            codes, scales = h_q[g]
            cols = slice(c * N + nt * P, c * N + (nt + 1) * P)
            nc.tensor.matmul_mx(out=bank, lhsT=n_q[0][:, cols].bitcast(FP8X4), lhsT_scale=n_q[1][:, cols],
                                rhs=codes[:, c, :].bitcast(FP8X4), rhs_scale=scales[:, c, :], start=start, stop=stop)

        def score(g, b):
            W = len(GROUPS[g]) * P
            j0 = GROUPS[g][0] * P
            bank = psum.tile([P, 2, W], F32, name=f"y_bank{g}", offset=b * BANK)
            for c in range(2):
                for nt in range(2):
                    score_pass(bank[:, nt, :], g, c, nt, c == 0 and nt == 0, c == 1 and nt == 1)
            y = keep.tile([P, 2, W], F32, name=f"y{g}")
            nc.scalar.copy(y[:], bank[:])
            nc.sync.dma_start(out=out.rearrange("(nt p) j -> p nt j", p=P)[:, :, j0 : j0 + W], in_=y[:])

        def score_last(b0, b1):
            banks = [psum.tile([P, 2 * P], F32, name=f"y_last{nt}", offset=(b0, b1)[nt] * BANK) for nt in range(2)]
            for c in range(2):
                for nt in range(2):
                    score_pass(banks[nt][:], 3, c, nt, c == 0, c == 1)
            for nt in range(2):
                y = keep.tile([P, 2 * P], F32, name=f"y_last_sb{nt}")
                if nt == 0:
                    nc.scalar.copy(y[:], banks[nt][:])
                else:
                    nc.vector.tensor_copy(y[:], banks[nt][:])
                (nc.scalar, nc.sync)[nt].dma_start(out=out[nt * P : (nt + 1) * P, J - 2 * P :], in_=y[:])

        entity(0, 0, 4)
        entity(0, 1, 5)
        entity(1, 0, 6)
        entity(1, 1, 4)
        entity(2, 0, 5)
        entity(2, 1, 6)
        entity(3, 0, 4)
        entity(3, 1, 5)
        deal_words(3)
        arr_out(1, 7)
        relation(0, 0, 0)
        relation(0, 1, 1)
        arr_out(3, 6)
        relation(1, 1, 2)
        relation(2, 0, 3)
        entity(4, 0, 7)
        entity(4, 1, 4)
        times_arr(1)
        times_arr(0)
        relation(2, 1, 0)
        arr_out(4, 5)
        entity(5, 0, 6)
        times_ari(0)
        relation(3, 1, 1)
        entity(5, 1, 7)
        entity(6, 0, 4)
        times_arr(3)
        times_ari(1)
        relation(4, 1, 2)
        entity(6, 1, 5)
        cast_n(0)
        turn(1, 0, 6)
        turn(1, 1, 7)
        times_arr(2)
        relation(5, 0, 3)
        entity(7, 0, 4)
        entity(7, 1, 5)
        times_arr(4)
        times_ari(2)
        relation(5, 1, 0)
        times_ari(3)
        relation(6, 0, 1)
        cast_n(1)
        turn(3, 0, 6)
        turn(3, 1, 7)
        times_ari(4)
        relation(6, 1, 2)
        add_on_gpsimd(0)
        times_arr(5)
        relation(7, 0, 3)
        turn(4, 0, 4)
        turn(4, 1, 5)
        times_ari(5)
        relation(7, 1, 0)
        add_on_gpsimd(2)
        turn(5, 0, 6)
        turn(5, 1, 7)
        times_arr(6)
        times_ari(6)
        turn(6, 0, 4)
        turn(6, 1, 5)
        times_arr(7)
        quantise_n()
        quantise(0)
        score(0, 1)
        quantise(1)
        score(1, 2)
        times_ari(7, 0)
        quantise(2)
        score(2, 6)
        times_ari(7, 1)
        add_on_vector(7, 0)
        quantise_last(6, 0)
        quantise_last(6, 1)
        add_on_vector(7, 1)
        quantise_last(7, 0)
        quantise_last(7, 1)
        score_last(1, 4)
